import numpy as np
import ml_dtypes


def mxq(x, axis, fmt="e4m3"):
    dtype, down = {"e4m3": (ml_dtypes.float8_e4m3fn, 7), "e5m2": (ml_dtypes.float8_e5m2, 14)}[fmt]
    v = np.moveaxis(np.asarray(x, np.float32).astype(ml_dtypes.bfloat16).astype(np.float64), axis, -1)
    blocks = v.reshape(v.shape[:-1] + (-1, 32))
    amax = np.abs(blocks).max(-1, keepdims=True)
    byte = np.maximum(np.where(amax > 0, np.frexp(amax)[1] - 1 + 127, 0) - down, 1)
    scale = np.exp2(byte - 127.0)
    codes = (blocks / scale).astype(np.float32).astype(dtype).astype(np.float64)
    return np.moveaxis((codes * scale).reshape(v.shape), -1, axis)


WIDE = False


def mx_kscale(k):
    if not WIDE:
        return np.ones(k)
    levels = np.array([10, -10, 5, -5, 0])
    if k % 512:
        return np.exp2(np.random.permutation(np.resize(levels, k // 32))).repeat(32)
    a = np.empty((k // 512, 16))
    for p in range(k // 512):
        a[p, :8] = np.random.permutation(np.resize(levels, 8))
        for g in range(8):
            far = levels[np.abs(levels - a[p, g]) >= 10]
            a[p, g + 8] = far[np.random.randint(len(far))]
    return np.exp2(a.ravel()).repeat(32)


BF16 = ml_dtypes.bfloat16


def bf(x):
    return np.asarray(x, np.float32).astype(BF16)


def f64(x):
    return np.asarray(x).astype(np.float64)

def planes(Y):
    n, m = Y.shape
    b = f64(bf(Y)).reshape(n // 32, 32, m)
    amax = np.abs(b).max(1)
    byte = np.clip(np.where(amax > 0, np.frexp(amax)[1] - 1 + 127 - 7, 1), 1, 254)
    codes = (b * np.exp2(127.0 - byte)[:, None, :]).reshape(n, m).astype(np.float32).astype(ml_dtypes.float8_e4m3fn).view(np.uint8)
    words = codes.reshape(n // 512, 128, 4, m).transpose(0, 1, 3, 2)
    return np.ascontiguousarray(words), np.ascontiguousarray(byte.astype(np.uint8).reshape(n // 512, 16, m))


B, N, E, C = 2048, 1024, 512, 512


def metric_distance(q, c, g, h):
    qg = q * g[None, :]
    ch = c * h[None, :]
    cross = mxq(qg, 1, "e4m3") @ mxq(ch, 1, "e4m3").T
    gh = g * h
    q2 = np.sum(gh[None, :] * np.square(q), axis=1)
    c2 = np.sum(gh[None, :] * np.square(c), axis=1)
    return np.sqrt(q2[:, None] + c2[None, :] - 2.0 * cross)


def row_softmax(logit):
    shifted = logit - np.max(logit, axis=1, keepdims=True)
    e = np.exp(shifted)
    return e / np.sum(e, axis=1, keepdims=True)


def setup_inputs():
    s, t = mx_kscale(E), mx_kscale(N)
    return {
        "q": bf(np.random.standard_normal((B, E))),
        "c": bf(np.random.standard_normal((N, E))),
        "g": bf((1.0 + 0.1 * np.random.standard_normal(E)) * s),
        "h": bf((1.0 + 0.1 * np.random.standard_normal(E)) / s),
        "y": bf(np.random.standard_normal((N, C)) / t[:, None]),
        "u": bf(np.random.uniform(size=N)),
        "r": bf(4.0 * np.random.standard_normal(N) * t),
    }


def core(q, c, g, h, y, u, r):
    q, c, g, h, y, u, r = f64(q), f64(c), f64(g), f64(h), f64(y), f64(u), f64(r)
    dist = metric_distance(q, c, g, h)
    keep = u < 0.7
    logit = np.where(keep[None, :], -2.0 * dist, -1e9)
    a = row_softmax(logit)
    ar = a * r[None, :]
    return mxq(ar, 1, "e4m3") @ mxq(y, 0, "e4m3")


def reference(q, c, g, h, y, u, r):
    R_out = core(q, c, g, h, y, u, r)
    words, scales = planes(R_out.T)
    return R_out, words, scales

@@ -1,0 +1,500 @@
+from contextlib import ExitStack
+
+import concourse.mybir as mybir
+from concourse.masks import make_identity
+
+F32 = mybir.dt.float32
+BF16 = mybir.dt.bfloat16
+U32 = mybir.dt.uint32
+I32 = mybir.dt.int32
+U8 = mybir.dt.uint8
+FP8X4 = mybir.dt.float8_e4m3fn_x4
+ALU = mybir.AluOpType
+ACT = mybir.ActivationFunctionType
+
+B, N, E, C = 2048, 1024, 512, 512
+P = 128
+NT = B // P
+FLOPS = 2 * B * N * E + 2 * B * N * C
+
+FAR = 2.5e17
+TINY = 1e-12
+SPOT = 1.5
+
+
+def tile_modernncastochasticneighbourregressor_x1_kernel(tc, q, c, g, h, y, u, r, out_0, out_1, out_2):
+    nc = tc.nc
+    with ExitStack() as ctx:
+        keep = ctx.enter_context(tc.tile_pool(name="keep", bufs=1))
+        xs = ctx.enter_context(tc.tile_pool(name="xs", bufs=NT))
+        work = ctx.enter_context(tc.tile_pool(name="work", bufs=3))
+        mm = ctx.enter_context(tc.psum_pool(name="mm", bufs=7))
+        qp = ctx.enter_context(tc.psum_pool(name="qp", bufs=1))
+
+        ident = keep.tile([P, P], F32, name="ident")
+        make_identity(nc, ident[:])
+        ones = keep.tile([P, P], BF16, name="ones")
+        rows = keep.tile([P, 2 * N], BF16, name="rows")
+        g4 = keep.tile([P, 4], BF16, name="g4")
+        h8 = keep.tile([P, 8], BF16, name="h8")
+        gh = keep.tile([P, 4], F32, name="gh")
+        craw = keep.tile([P, 2, 4, E], BF16, name="craw")
+        yraw = keep.tile([P, 2, 4, C], BF16, name="yraw")
+        qraw = keep.tile([P, NT, E], BF16, name="qraw")
+        big = keep.tile([P, N], F32, name="big")
+        r_b = keep.tile([P, N], F32, name="r_b")
+        c2m = keep.tile([P, N], F32, name="c2m")
+        csq = [keep.tile([P, 4, 512], F32, name="csq%d" % i) for i in range(2)]
+        ch_codes = keep.tile([P, N], U32, name="ch_codes", align_bytes=64)
+        ch_scales = keep.tile([P, N], U8, name="ch_scales", align_bytes=64)
+        q_codes = keep.tile([P, B], U32, name="q_codes", align_bytes=64)
+        q_scales = keep.tile([P, B], U8, name="q_scales", align_bytes=64)
+        yg = keep.tile([P, 2, 4 * C], BF16, name="yg", align_bytes=64)
+        y_codes = keep.tile([P, 2, C], U32, name="y_codes", align_bytes=64)
+        y_scales = keep.tile([P, 2, C], U8, name="y_scales", align_bytes=64)
+        o_scales = keep.tile([P, B], U8, name="o_scales", align_bytes=64)
+        q2ps = qp.tile([P, NT], F32, name="q2ps")
+        q2 = keep.tile([P, NT], F32, name="q2")
+        xmin = keep.tile([P, NT], F32, name="xmin")
+        xm = keep.tile([P, NT], F32, name="xm")
+        rk = keep.tile([P, NT], F32, name="rk")
+        w2 = keep.tile([P, NT], F32, name="w2")
+        nw = keep.tile([P, NT], F32, name="nw")
+        shift = keep.tile([P, NT], F32, name="shift")
+        ssum = keep.tile([P, NT], F32, name="ssum")
+        rs = keep.tile([P, NT], F32, name="rs")
+        x = [xs.tile([P, N], F32, name="x") for i in range(NT)]
+
+        ctx.enter_context(tc.manual_schedule())
+
+        nc.vector.memset(rows[:].bitcast(I32), 0)
+        nc.vector.memset(ones[:], 1.0)
+        nc.scalar.dma_start(out=h8[:, 0:4], in_=h.rearrange("(p t) -> p t", t=4))
+        nc.scalar.dma_start(out=g4[:], in_=g.rearrange("(p t) -> p t", t=4))
+        nc.scalar.dma_start(out=rows[0:1, 0:N], in_=u.unsqueeze(0))
+        nc.scalar.dma_start(out=rows[0:1, N : 2 * N], in_=r.unsqueeze(0))
+        c_view = c.rearrange("(a p t) d -> a p t d", a=2, t=4)
+        q_view = q.rearrange("(k p) d -> p k d", p=P)
+        y_view = y.rearrange("(a p t) d -> a p t d", a=2, t=4)
+        for a in range(2):
+            for v in range(2):
+                nc.sync.dma_start(out=craw[:, a, 2 * v : 2 * v + 2, :], in_=c_view[a, :, 2 * v : 2 * v + 2, :])
+        for j in range(NT // 2):
+            nc.sync.dma_start(out=qraw[:, 2 * j : 2 * j + 2, :], in_=q_view[:, 2 * j : 2 * j + 2, :])
+        for a in range(2):
+            nc.sync.dma_start(out=yraw[:, a, :, :], in_=y_view[a])
+
+        nc.vector.tensor_copy(out=h8[:, 4:8], in_=h8[:, 0:4])
+        nc.vector.tensor_tensor(out=gh[:], in0=g4[:], in1=h8[:, 0:4], op=ALU.mult)
+
+        trs = {}
+
+        def c_turn(a, v):
+            t = mm.tile([P, 512], F32, name="bank")
+            trs["c", a, v] = t
+            for e in range(2):
+                words = craw[:, a, 2 * v + e, :].bitcast(F32)
+                for w in range(2):
+                    s = (2 * e + w) * P
+                    nc.tensor.transpose(t[:, s : s + P], words[:, w : E // 2 : 2], ident[:])
+
+        chgs = {}
+
+        def c_scale(a, v):
+            b16 = trs["c", a, v][:].bitcast(BF16)
+            chg = work.tile([P, 1024], BF16, name="grp", align_bytes=64)
+            chgs[a, v] = chg
+            nc.vector.tensor_tensor(
+                out=chg[:].rearrange("p (c x d) -> p c x d", x=4, d=2),
+                in0=b16.rearrange("p (x c d) -> p c x d", x=4, d=2),
+                in1=h8[:].rearrange("p (x d) -> p x d", d=2).unsqueeze(1).to_broadcast([P, P, 4, 2]),
+                op=ALU.mult,
+            )
+
+        def c_square(a, v):
+            b16 = trs["c", a, v][:].bitcast(BF16).rearrange("p (e w c d) -> p w e c d", e=2, w=2, d=2)
+            for d in range(2):
+                nc.scalar.activation(
+                    out=csq[a][:, d:4:2, 256 * v : 256 * v + 256].rearrange("p w (e c) -> p w e c", e=2),
+                    in_=b16[:, :, :, :, d],
+                    func=ACT.Square,
+                )
+
+        def c_quant(a, v):
+            s = slice(512 * a + 256 * v, 512 * a + 256 * v + 256)
+            nc.vector.quantize_mx(out=ch_codes[:, s].bitcast(FP8X4), scales=ch_scales[:, s], in_=chgs[a, v][:])
+
+        c2ps = {}
+
+        def c_sum(a):
+            t = mm.tile([P, 512], F32, name="bank")
+            c2ps[a] = t
+            for s in range(4):
+                nc.tensor.matmul(
+                    t[:], lhsT=gh[:, s : s + 1].to_broadcast([P, P]), rhs=csq[a][:, s, :], start=(s == 0), stop=(s == 3)
+                )
+
+        def c_mask(a):
+            s = slice(512 * a, 512 * a + 512)
+            nc.vector.tensor_tensor(
+                out=c2m[:, s].rearrange("p (v c e) -> p v c e", v=2, e=2),
+                in0=c2ps[a][:].rearrange("p (v e c) -> p v c e", v=2, e=2),
+                in1=big[:, s].rearrange("p (v c e) -> p v c e", v=2, e=2),
+                op=ALU.add,
+            )
+
+        def q_turn(j):
+            t = mm.tile([P, 512], F32, name="bank")
+            trs["q", j] = t
+            for w in range(2):
+                for k in range(2):
+                    s = w * 256 + k * P
+                    nc.tensor.transpose(t[:, s : s + P], qraw[:, 2 * j + k, :].bitcast(F32)[:, w : E // 2 : 2], ident[:])
+
+        qgs = {}
+
+        def q_scale(j):
+            b16 = trs["q", j][:].bitcast(BF16)
+            qg = work.tile([P, 1024], BF16, name="grp", align_bytes=64)
+            qgs[j] = qg
+            nc.vector.tensor_tensor(
+                out=qg[:].rearrange("p (r w d) -> p r w d", w=2, d=2),
+                in0=b16.rearrange("p (w r d) -> p r w d", w=2, d=2),
+                in1=g4[:].rearrange("p (w d) -> p w d", d=2).unsqueeze(1).to_broadcast([P, 256, 2, 2]),
+                op=ALU.mult,
+            )
+
+        qsqs = {}
+
+        def q_square(j):
+            b16 = trs["q", j][:].bitcast(BF16).rearrange("p (w r d) -> p w r d", w=2, d=2)
+            qsq = work.tile([P, 4, 256], F32, name="qsq")
+            qsqs[j] = qsq
+            for d in range(2):
+                nc.scalar.activation(out=qsq[:, d:4:2, :], in_=b16[:, :, :, d], func=ACT.Square)
+
+        def q_quant(j):
+            s = slice(256 * j, 256 * j + 256)
+            nc.vector.quantize_mx(out=q_codes[:, s].bitcast(FP8X4), scales=q_scales[:, s], in_=qgs[j][:])
+
+        def q_sum(j):
+            for k in range(2):
+                i = 2 * j + k
+                for s in range(4):
+                    nc.tensor.matmul(
+                        q2ps[:, i : i + 1],
+                        lhsT=qsqs[j][:, s, k * P : k * P + P],
+                        rhs=gh[:, s : s + 1],
+                        start=(s == 0),
+                        stop=(s == 3),
+                    )
+
+        def q_keep(j):
+            nc.scalar.copy(out=q2[:, 2 * j : 2 * j + 2], in_=q2ps[:, 2 * j : 2 * j + 2])
+
+        crosses = {}
+
+        def cross(i, n):
+            t = mm.tile([P, 512], F32, name="bank")
+            crosses[i, n] = t
+            b = slice(P * i, P * i + P)
+            s = slice(512 * n, 512 * n + 512)
+            nc.tensor.matmul_mx(
+                out=t[:],
+                lhsT=q_codes[:, b].bitcast(FP8X4),
+                lhsT_scale=q_scales[:, b],
+                rhs=ch_codes[:, s].bitcast(FP8X4),
+                rhs_scale=ch_scales[:, s],
+                start=True,
+                stop=True,
+            )
+
+        def add_c2(i, n):
+            s = slice(512 * n, 512 * n + 512)
+            nc.vector.scalar_tensor_tensor(
+                out=x[i][:, s], in0=crosses[i, n][:], scalar=-2.0, in1=c2m[:, s], op0=ALU.mult, op1=ALU.add
+            )
+
+        def add_q2(i):
+            nc.vector.tensor_scalar(
+                out=x[i][:],
+                in0=x[i][:],
+                scalar1=q2[:, i : i + 1],
+                scalar2=None,
+                op0=ALU.add,
+                op1=ALU.min,
+                accum_out=xmin[:, i : i + 1],
+            )
+
+        def row_a(s):
+            nc.gpsimd.tensor_scalar(
+                out=xm[:, s], in0=xmin[:, s], scalar1=TINY, scalar2=1.0 / SPOT, op0=ALU.max, op1=ALU.mult
+            )
+
+        def row_b(s):
+            nc.vector.reciprocal(out=rk[:, s], in_=xm[:, s])
+
+        def row_c(s):
+            nc.scalar.activation(out=w2[:, s], in_=xm[:, s], func=ACT.Sqrt, scale=4.0)
+            nc.gpsimd.tensor_scalar(out=nw[:, s], in0=w2[:, s], scalar1=-1.0, scalar2=0.0, op0=ALU.mult, op1=ALU.add)
+            nc.gpsimd.tensor_scalar(
+                out=shift[:, s], in0=w2[:, s], scalar1=SPOT**0.5, scalar2=0.0, op0=ALU.mult, op1=ALU.add
+            )
+
+        def root(i):
+            nc.scalar.activation(out=x[i][:], in_=x[i][:], func=ACT.Sqrt, scale=rk[:, i : i + 1])
+
+        def y_group(a):
+            nc.vector.tensor_copy(
+                out=yg[:, a, :].rearrange("p (t c j) -> p t c j", t=4, j=4),
+                in_=yraw[:, a, :, :].rearrange("p j (c t) -> p t c j", t=4),
+            )
+
+        def y_quant(a):
+            nc.vector.quantize_mx(out=y_codes[:, a, :].bitcast(FP8X4), scales=y_scales[:, a, :], in_=yg[:, a, :])
+
+        ub = {}
+
+        def spread(a):
+            ub[a] = mm.tile([P, 512], F32, name="bank")
+            nc.tensor.matmul(ub[a][:], lhsT=ones[:], rhs=rows[:, 512 * a : 512 * a + 512], start=True, stop=True)
+
+        def far(a):
+            nc.vector.tensor_scalar(
+                out=big[:, 512 * a : 512 * a + 512].rearrange("p (v c e) -> p v c e", v=2, e=2),
+                in0=ub[a][:].rearrange("p (c v e) -> p v c e", v=2, e=2),
+                scalar1=0.7,
+                scalar2=FAR,
+                op0=ALU.is_ge,
+                op1=ALU.mult,
+            )
+
+        def gain(a):
+            nc.scalar.copy(
+                out=r_b[:, 512 * a : 512 * a + 512].rearrange("p (v c e) -> p v c e", v=2, e=2),
+                in_=ub[2 + a][:].rearrange("p (c v e) -> p v c e", v=2, e=2),
+            )
+
+        order = [(0, 0), (0, 1), (1, 0), (1, 1)]
+        spread(0)
+        spread(1)
+        for k in range(4):
+            c_turn(*order[k])
+        far(0)
+        far(1)
+        for k in range(4):
+            c_scale(*order[k])
+            c_square(*order[k])
+            if k:
+                c_quant(*order[k - 1])
+        q_turn(0)
+        q_turn(1)
+        c_sum(0)
+        q_scale(0)
+        c_quant(1, 1)
+        q_square(0)
+        q_turn(2)
+        q_scale(1)
+        q_quant(0)
+        q_square(1)
+        c_mask(0)
+        q_quant(1)
+        cross(0, 0)
+        cross(1, 0)
+        cross(2, 0)
+        c_sum(1)
+        q_scale(2)
+        q_square(2)
+        add_c2(0, 0)
+        q_quant(2)
+        add_c2(1, 0)
+        cross(3, 0)
+        q_turn(3)
+        q_sum(0)
+        q_keep(0)
+        add_c2(2, 0)
+        add_c2(3, 0)
+        q_scale(3)
+        q_square(3)
+        c_mask(1)
+        q_quant(3)
+        cross(0, 1)
+        cross(1, 1)
+        q_turn(4)
+
+        NP = NT // 2
+        for i in range(NT):
+            if i < 4:
+                if i + 2 < 4:
+                    cross(i + 2, 1)
+                add_c2(i, 1)
+            else:
+                add_c2(i, 0)
+                add_c2(i, 1)
+            if 2 <= i < NT - 2:
+                cross(i + 2, 0)
+                cross(i + 2, 1)
+            if i % 2 == 0 and 1 + i // 2 < NP:
+                q_sum(1 + i // 2)
+            if i:
+                add_q2(i - 1)
+            j = 4 + i // 2
+            if i % 2 == 0 and j < NP:
+                q_scale(j)
+                q_square(j)
+            if i % 2 == 1 and j < NP:
+                q_quant(j)
+                if j + 1 < NP:
+                    q_turn(j + 1)
+            if i % 2 == 0 and 1 + i // 2 < NP:
+                q_keep(1 + i // 2)
+            if i % 2 == 0 and i:
+                s = slice(i - 2, i)
+                row_a(s)
+            if i % 2 == 1 and i > 1:
+                s = slice(i - 3, i - 1)
+                row_b(s)
+                row_c(s)
+                root(i - 3)
+                root(i - 2)
+            if i == 9:
+                spread(2)
+                gain(0)
+                spread(3)
+                gain(1)
+        row_a(slice(NT - 2, NT - 1))
+        add_q2(NT - 1)
+        row_b(slice(NT - 2, NT - 1))
+        row_c(slice(NT - 2, NT - 1))
+        root(NT - 2)
+        row_a(slice(NT - 1, NT))
+        y_group(0)
+        row_b(slice(NT - 1, NT))
+        row_c(slice(NT - 1, NT))
+        root(NT - 1)
+        y_group(1)
+        y_quant(0)
+        y_quant(1)
+
+        ars, arts, outs = {}, {}, {}
+        art_codes, art_scales = {}, {}
+        ocs = {}
+        ogs = {}
+
+        def expo(i):
+            nc.scalar.activation(
+                out=x[i][:],
+                in_=x[i][:],
+                func=ACT.Exp,
+                scale=nw[:, i : i + 1],
+                bias=shift[:, i : i + 1],
+                accum_out=ssum[:, i : i + 1],
+            )
+
+        def inv(i):
+            nc.vector.reciprocal(out=rs[:, i : i + 1], in_=ssum[:, i : i + 1])
+
+        def weigh(i):
+            t = work.tile([P, N], BF16, name="ar", align_bytes=64)
+            ars[i] = t
+            nc.vector.scalar_tensor_tensor(
+                out=t[:], in0=x[i][:], scalar=rs[:, i : i + 1], in1=r_b[:], op0=ALU.mult, op1=ALU.mult
+            )
+
+        def turn(i):
+            t = mm.tile([P, 512], F32, name="bank")
+            trs["a", i] = t
+            words = ars[i][:].bitcast(F32)
+            for k in range(4):
+                nc.tensor.transpose(t[:, P * k : P * k + P], words[:, P * k : P * k + P], ident[:])
+
+        def unpack(i):
+            t = work.tile([P, 1024], BF16, name="art", align_bytes=64)
+            arts[i] = t
+            nc.vector.tensor_copy(
+                out=t[:].bitcast(F32).rearrange("p (a b v) -> p a b v", a=2, v=2),
+                in_=trs["a", i][:].rearrange("p (a v b) -> p a b v", a=2, v=2),
+            )
+
+        def a_quant(i):
+            k = work.tile([P, 256], U32, name="art_codes", align_bytes=64)
+            s = work.tile([P, 256], U8, name="art_scales", align_bytes=64)
+            art_codes[i], art_scales[i] = k, s
+            nc.vector.quantize_mx(out=k[:].bitcast(FP8X4), scales=s[:], in_=arts[i][:])
+
+        def second(i):
+            t = mm.tile([P, 512], F32, name="bank")
+            tt = mm.tile([P, 512], F32, name="bank")
+            outs[i] = (t, tt)
+            k, s = art_codes[i], art_scales[i]
+            for a in range(2):
+                nc.tensor.matmul_mx(
+                    out=t[:],
+                    lhsT=k[:, P * a : P * a + P].bitcast(FP8X4),
+                    lhsT_scale=s[:, P * a : P * a + P],
+                    rhs=y_codes[:, a, :].bitcast(FP8X4),
+                    rhs_scale=y_scales[:, a, :],
+                    start=(a == 0),
+                    stop=(a == 1),
+                )
+            for m in range(4):
+                for a in range(2):
+                    nc.tensor.matmul_mx(
+                        out=tt[:, P * m : P * m + P],
+                        lhsT=y_codes[:, a, P * m : P * m + P].bitcast(FP8X4),
+                        lhsT_scale=y_scales[:, a, P * m : P * m + P],
+                        rhs=k[:, P * a : P * a + P].bitcast(FP8X4),
+                        rhs_scale=s[:, P * a : P * a + P],
+                        start=(a == 0),
+                        stop=(a == 1),
+                    )
+
+        def leave(i):
+            t = work.tile([P, C], F32, name="o")
+            nc.scalar.copy(
+                out=t[:].rearrange("p (c m) -> p c m", m=4), in_=outs[i][0][:].rearrange("p (m c) -> p c m", m=4)
+            )
+            nc.sync.dma_start(out=out_0[P * i : P * i + P, :], in_=t[:])
+
+        def leave_t(i):
+            if i % 2 == 0:
+                og = work.tile([P, 1024], BF16, name="og", align_bytes=64)
+                ogs[i // 2] = og
+            nc.scalar.copy(
+                out=ogs[i // 2][:, 512 * (i % 2) : 512 * (i % 2) + 512].rearrange("p (b m) -> p b m", m=4),
+                in_=outs[i][1][:].rearrange("p (m b) -> p b m", m=4),
+            )
+
+        def o_quant(j):
+            k = work.tile([P, 256], U32, name="o_codes", align_bytes=64)
+            s = slice(256 * j, 256 * j + 256)
+            nc.vector.quantize_mx(out=k[:].bitcast(FP8X4), scales=o_scales[:, s], in_=ogs[j][:])
+            nc.sync.dma_start(
+                out=out_1[0, :, s, :].rearrange("p m t -> p (m t)").bitcast(I32), in_=k[:].bitcast(I32)
+            )
+            if j % 4 == 3:
+                s = slice(256 * (j - 3), 256 * j + 256)
+                for b in range(4):
+                    nc.sync.dma_start(
+                        out=out_2[0, 4 * b : 4 * b + 4, s].bitcast(I32), in_=o_scales[32 * b : 32 * b + 4, s].bitcast(I32)
+                    )
+
+        expo(0)
+        for i in range(NT + 4):
+            if i + 1 < NT:
+                expo(i + 1)
+            if i < NT:
+                inv(i)
+            if 3 <= i <= NT + 2:
+                leave(i - 3)
+                leave_t(i - 3)
+            if 2 <= i <= NT + 1:
+                a_quant(i - 2)
+                second(i - 2)
+            if i < NT:
+                weigh(i)
+                turn(i)
+            if i >= 4 and i % 2 == 0:
+                o_quant((i - 4) // 2)
+            if 1 <= i <= NT:
+                unpack(i - 1)

@@ -15,11 +15,17 @@ ACT = mybir.ActivationFunctionType
 B, N, E, C = 2048, 1024, 512, 512
 P = 128
 NT = B // P
+NP = NT // 2
 FLOPS = 2 * B * N * E + 2 * B * N * C
 
 FAR = 2.5e17
 TINY = 1e-12
 SPOT = 1.5
+H = 8
+LEAVE_V = [6,8,10]
+LEAVE_T_V = []
+SCALE_V = []
+KEEP_S = False
 
 
 def tile_modernncastochasticneighbourregressor_x1_kernel(tc, q, c, g, h, y, u, r, out_0, out_1, out_2):
@@ -28,23 +34,20 @@ def tile_modernncastochasticneighbourregressor_x1_kernel(tc, q, c, g, h, y, u, r
         keep = ctx.enter_context(tc.tile_pool(name="keep", bufs=1))
         xs = ctx.enter_context(tc.tile_pool(name="xs", bufs=NT))
         work = ctx.enter_context(tc.tile_pool(name="work", bufs=3))
-        mm = ctx.enter_context(tc.psum_pool(name="mm", bufs=7))
+        mm = ctx.enter_context(tc.psum_pool(name="mm", bufs=2))
         qp = ctx.enter_context(tc.psum_pool(name="qp", bufs=1))
 
         ident = keep.tile([P, P], F32, name="ident")
-        make_identity(nc, ident[:])
-        ones = keep.tile([P, P], BF16, name="ones")
-        rows = keep.tile([P, 2 * N], BF16, name="rows")
         g4 = keep.tile([P, 4], BF16, name="g4")
-        h8 = keep.tile([P, 8], BF16, name="h8")
+        h4 = keep.tile([P, 4], BF16, name="h4")
         gh = keep.tile([P, 4], F32, name="gh")
+        u8 = keep.tile([P, 2, 4], BF16, name="u8")
+        r8 = keep.tile([P, 2, 4], BF16, name="r8")
+        far = keep.tile([P, 8], F32, name="far")
         craw = keep.tile([P, 2, 4, E], BF16, name="craw")
         yraw = keep.tile([P, 2, 4, C], BF16, name="yraw")
         qraw = keep.tile([P, NT, E], BF16, name="qraw")
-        big = keep.tile([P, N], F32, name="big")
-        r_b = keep.tile([P, N], F32, name="r_b")
         c2m = keep.tile([P, N], F32, name="c2m")
-        csq = [keep.tile([P, 4, 512], F32, name="csq%d" % i) for i in range(2)]
         ch_codes = keep.tile([P, N], U32, name="ch_codes", align_bytes=64)
         ch_scales = keep.tile([P, N], U8, name="ch_scales", align_bytes=64)
         q_codes = keep.tile([P, B], U32, name="q_codes", align_bytes=64)
@@ -53,8 +56,9 @@ def tile_modernncastochasticneighbourregressor_x1_kernel(tc, q, c, g, h, y, u, r
         y_codes = keep.tile([P, 2, C], U32, name="y_codes", align_bytes=64)
         y_scales = keep.tile([P, 2, C], U8, name="y_scales", align_bytes=64)
         o_scales = keep.tile([P, B], U8, name="o_scales", align_bytes=64)
-        q2ps = qp.tile([P, NT], F32, name="q2ps")
+        sums = qp.tile([P, NT + 8], F32, name="sums")
         q2 = keep.tile([P, NT], F32, name="q2")
+        c2 = keep.tile([P, 8], F32, name="c2")
         xmin = keep.tile([P, NT], F32, name="xmin")
         xm = keep.tile([P, NT], F32, name="xm")
         rk = keep.tile([P, NT], F32, name="rk")
@@ -67,136 +71,137 @@ def tile_modernncastochasticneighbourregressor_x1_kernel(tc, q, c, g, h, y, u, r
 
         ctx.enter_context(tc.manual_schedule())
 
-        nc.vector.memset(rows[:].bitcast(I32), 0)
-        nc.vector.memset(ones[:], 1.0)
-        nc.scalar.dma_start(out=h8[:, 0:4], in_=h.rearrange("(p t) -> p t", t=4))
+        nc.scalar.dma_start(out=h4[:], in_=h.rearrange("(p t) -> p t", t=4))
         nc.scalar.dma_start(out=g4[:], in_=g.rearrange("(p t) -> p t", t=4))
-        nc.scalar.dma_start(out=rows[0:1, 0:N], in_=u.unsqueeze(0))
-        nc.scalar.dma_start(out=rows[0:1, N : 2 * N], in_=r.unsqueeze(0))
+        nc.scalar.dma_start(out=u8[:], in_=u.rearrange("(a p t) -> p a t", a=2, t=4))
+        nc.scalar.dma_start(out=r8[:], in_=r.rearrange("(a p t) -> p a t", a=2, t=4))
+        make_identity(nc, ident[:])
         c_view = c.rearrange("(a p t) d -> a p t d", a=2, t=4)
         q_view = q.rearrange("(k p) d -> p k d", p=P)
         y_view = y.rearrange("(a p t) d -> a p t d", a=2, t=4)
         for a in range(2):
             for v in range(2):
                 nc.sync.dma_start(out=craw[:, a, 2 * v : 2 * v + 2, :], in_=c_view[a, :, 2 * v : 2 * v + 2, :])
-        for j in range(NT // 2):
+        for j in range(NP):
             nc.sync.dma_start(out=qraw[:, 2 * j : 2 * j + 2, :], in_=q_view[:, 2 * j : 2 * j + 2, :])
-        for a in range(2):
-            nc.sync.dma_start(out=yraw[:, a, :, :], in_=y_view[a])
+            if j == 3:
+                for a in range(2):
+                    nc.sync.dma_start(out=yraw[:, a, :, :], in_=y_view[a])
+        nc.vector.tensor_tensor(out=gh[:], in0=g4[:], in1=h4[:], op=ALU.mult)
+        nc.vector.tensor_scalar(
+            out=far[:],
+            in0=u8[:].rearrange("p a t -> p (a t)"),
+            scalar1=0.7,
+            scalar2=FAR,
+            op0=ALU.is_ge,
+            op1=ALU.mult,
+        )
 
-        nc.vector.tensor_copy(out=h8[:, 4:8], in_=h8[:, 0:4])
-        nc.vector.tensor_tensor(out=gh[:], in0=g4[:], in1=h8[:, 0:4], op=ALU.mult)
+        tiles = {}
 
-        trs = {}
+        depth = {"x": 3, "o": 4}
 
-        def c_turn(a, v):
-            t = mm.tile([P, 512], F32, name="bank")
-            trs["c", a, v] = t
-            for e in range(2):
-                words = craw[:, a, 2 * v + e, :].bitcast(F32)
-                for w in range(2):
-                    s = (2 * e + w) * P
-                    nc.tensor.transpose(t[:, s : s + P], words[:, w : E // 2 : 2], ident[:])
+        def bank(tag, *key):
+            t = mm.tile([P, 512], F32, name=tag, bufs=depth[tag])
+            tiles[key] = t
+            return t
 
-        chgs = {}
+        def head_bank(*key):
+            return bank("o", *key)
 
-        def c_scale(a, v):
-            b16 = trs["c", a, v][:].bitcast(BF16)
-            chg = work.tile([P, 1024], BF16, name="grp", align_bytes=64)
-            chgs[a, v] = chg
-            nc.vector.tensor_tensor(
-                out=chg[:].rearrange("p (c x d) -> p c x d", x=4, d=2),
-                in0=b16.rearrange("p (x c d) -> p c x d", x=4, d=2),
-                in1=h8[:].rearrange("p (x d) -> p x d", d=2).unsqueeze(1).to_broadcast([P, P, 4, 2]),
-                op=ALU.mult,
-            )
-
-        def c_square(a, v):
-            b16 = trs["c", a, v][:].bitcast(BF16).rearrange("p (e w c d) -> p w e c d", e=2, w=2, d=2)
-            for d in range(2):
-                nc.scalar.activation(
-                    out=csq[a][:, d:4:2, 256 * v : 256 * v + 256].rearrange("p w (e c) -> p w e c", e=2),
-                    in_=b16[:, :, :, :, d],
-                    func=ACT.Square,
-                )
-
-        def c_quant(a, v):
-            s = slice(512 * a + 256 * v, 512 * a + 256 * v + 256)
-            nc.vector.quantize_mx(out=ch_codes[:, s].bitcast(FP8X4), scales=ch_scales[:, s], in_=chgs[a, v][:])
-
-        c2ps = {}
-
-        def c_sum(a):
-            t = mm.tile([P, 512], F32, name="bank")
-            c2ps[a] = t
-            for s in range(4):
-                nc.tensor.matmul(
-                    t[:], lhsT=gh[:, s : s + 1].to_broadcast([P, P]), rhs=csq[a][:, s, :], start=(s == 0), stop=(s == 3)
-                )
-
-        def c_mask(a):
-            s = slice(512 * a, 512 * a + 512)
-            nc.vector.tensor_tensor(
-                out=c2m[:, s].rearrange("p (v c e) -> p v c e", v=2, e=2),
-                in0=c2ps[a][:].rearrange("p (v e c) -> p v c e", v=2, e=2),
-                in1=big[:, s].rearrange("p (v c e) -> p v c e", v=2, e=2),
-                op=ALU.add,
-            )
-
-        def q_turn(j):
-            t = mm.tile([P, 512], F32, name="bank")
-            trs["q", j] = t
+        def turn_rows(key, rows):
+            t = head_bank(*key)
             for w in range(2):
                 for k in range(2):
                     s = w * 256 + k * P
-                    nc.tensor.transpose(t[:, s : s + P], qraw[:, 2 * j + k, :].bitcast(F32)[:, w : E // 2 : 2], ident[:])
+                    nc.tensor.transpose(t[:, s : s + P], rows[k].bitcast(F32)[:, w : E // 2 : 2], ident[:])
 
-        qgs = {}
-
-        def q_scale(j):
-            b16 = trs["q", j][:].bitcast(BF16)
-            qg = work.tile([P, 1024], BF16, name="grp", align_bytes=64)
-            qgs[j] = qg
+        def scale_rows(key, factor):
+            t = work.tile([P, 1024], BF16, name="grp", align_bytes=64)
+            tiles["grp", key] = t
             nc.vector.tensor_tensor(
-                out=qg[:].rearrange("p (r w d) -> p r w d", w=2, d=2),
-                in0=b16.rearrange("p (w r d) -> p r w d", w=2, d=2),
-                in1=g4[:].rearrange("p (w d) -> p w d", d=2).unsqueeze(1).to_broadcast([P, 256, 2, 2]),
+                out=t[:].rearrange("p (r w d) -> p r w d", w=2, d=2),
+                in0=tiles[key][:].bitcast(BF16).rearrange("p (w r d) -> p r w d", w=2, d=2),
+                in1=factor[:].rearrange("p (w d) -> p w d", d=2).unsqueeze(1).to_broadcast([P, 256, 2, 2]),
                 op=ALU.mult,
             )
 
-        qsqs = {}
-
-        def q_square(j):
-            b16 = trs["q", j][:].bitcast(BF16).rearrange("p (w r d) -> p w r d", w=2, d=2)
-            qsq = work.tile([P, 4, 256], F32, name="qsq")
-            qsqs[j] = qsq
+        def square_rows(key):
+            b16 = tiles[key][:].bitcast(BF16).rearrange("p (w r d) -> p w r d", w=2, d=2)
+            t = work.tile([P, 4, 256], F32, name="sq", bufs=6)
+            tiles["sq", key] = t
             for d in range(2):
-                nc.scalar.activation(out=qsq[:, d:4:2, :], in_=b16[:, :, :, d], func=ACT.Square)
+                nc.scalar.activation(out=t[:, d:4:2, :], in_=b16[:, :, :, d], func=ACT.Square)
 
-        def q_quant(j):
-            s = slice(256 * j, 256 * j + 256)
-            nc.vector.quantize_mx(out=q_codes[:, s].bitcast(FP8X4), scales=q_scales[:, s], in_=qgs[j][:])
-
-        def q_sum(j):
+        def sum_rows(key, first):
             for k in range(2):
-                i = 2 * j + k
                 for s in range(4):
                     nc.tensor.matmul(
-                        q2ps[:, i : i + 1],
-                        lhsT=qsqs[j][:, s, k * P : k * P + P],
+                        sums[:, first + k : first + k + 1],
+                        lhsT=tiles["sq", key][:, s, k * P : k * P + P],
                         rhs=gh[:, s : s + 1],
                         start=(s == 0),
                         stop=(s == 3),
                     )
 
-        def q_keep(j):
-            nc.scalar.copy(out=q2[:, 2 * j : 2 * j + 2], in_=q2ps[:, 2 * j : 2 * j + 2])
+        def quantise(codes, scales, key, j):
+            s = slice(256 * j, 256 * j + 256)
+            nc.vector.quantize_mx(out=codes[:, s].bitcast(FP8X4), scales=scales[:, s], in_=tiles["grp", key][:])
 
-        crosses = {}
+        def c_turn(k):
+            turn_rows(("c", k), [craw[:, k // 2, 2 * (k % 2) + e, :] for e in range(2)])
+
+        def c_scale(k):
+            scale_rows(("c", k), h4)
+
+        def c_square(k):
+            square_rows(("c", k))
+
+        def c_quant(k):
+            quantise(ch_codes, ch_scales, ("c", k), k)
+
+        def c_col(k):
+            sum_rows(("c", k), NT + 2 * k)
+
+        def c_add(a):
+            s = slice(4 * a, 4 * a + 4)
+            nc.vector.tensor_tensor(out=c2[:, s], in0=sums[:, NT + 4 * a : NT + 4 * a + 4], in1=far[:, s], op=ALU.add)
+
+        def c_bcast(a):
+            t = bank("x", "c2", a)
+            for k in range(4):
+                nc.tensor.matmul(
+                    t[:, P * k : P * k + P],
+                    lhsT=c2[:, 4 * a + k : 4 * a + k + 1].to_broadcast([P, P]),
+                    rhs=ident[:],
+                    start=True,
+                    stop=True,
+                )
+
+        def c_keep(a):
+            copy = nc.scalar.copy if KEEP_S else nc.vector.tensor_copy
+            copy(out=c2m[:, 512 * a : 512 * a + 512], in_=tiles["c2", a][:])
+
+        def q_turn(j):
+            turn_rows(("q", j), [qraw[:, 2 * j + k, :] for k in range(2)])
+
+        def q_scale(j):
+            scale_rows(("q", j), g4)
+
+        def q_square(j):
+            square_rows(("q", j))
+
+        def q_quant(j):
+            quantise(q_codes, q_scales, ("q", j), j)
+
+        def q_sum(j):
+            sum_rows(("q", j), 2 * j)
+
+        def q_keep(j):
+            nc.vector.tensor_copy(out=q2[:, 2 * j : 2 * j + 2], in_=sums[:, 2 * j : 2 * j + 2])
 
         def cross(i, n):
-            t = mm.tile([P, 512], F32, name="bank")
-            crosses[i, n] = t
+            t = bank("x", "cross", i, n)
             b = slice(P * i, P * i + P)
             s = slice(512 * n, 512 * n + 512)
             nc.tensor.matmul_mx(
@@ -209,13 +214,13 @@ def tile_modernncastochasticneighbourregressor_x1_kernel(tc, q, c, g, h, y, u, r
                 stop=True,
             )
 
-        def add_c2(i, n):
+        def dist(i, n):
             s = slice(512 * n, 512 * n + 512)
             nc.vector.scalar_tensor_tensor(
-                out=x[i][:, s], in0=crosses[i, n][:], scalar=-2.0, in1=c2m[:, s], op0=ALU.mult, op1=ALU.add
+                out=x[i][:, s], in0=tiles["cross", i, n][:], scalar=-2.0, in1=c2m[:, s], op0=ALU.mult, op1=ALU.add
             )
 
-        def add_q2(i):
+        def low(i):
             nc.vector.tensor_scalar(
                 out=x[i][:],
                 in0=x[i][:],
@@ -226,15 +231,18 @@ def tile_modernncastochasticneighbourregressor_x1_kernel(tc, q, c, g, h, y, u, r
                 accum_out=xmin[:, i : i + 1],
             )
 
-        def row_a(s):
+        def row_a(i):
+            s = slice(i, i + 1)
             nc.gpsimd.tensor_scalar(
                 out=xm[:, s], in0=xmin[:, s], scalar1=TINY, scalar2=1.0 / SPOT, op0=ALU.max, op1=ALU.mult
             )
 
-        def row_b(s):
+        def row_b(i):
+            s = slice(i, i + 1)
             nc.vector.reciprocal(out=rk[:, s], in_=xm[:, s])
 
-        def row_c(s):
+        def row_c(i, m):
+            s = slice(i, i + m)
             nc.scalar.activation(out=w2[:, s], in_=xm[:, s], func=ACT.Sqrt, scale=4.0)
             nc.gpsimd.tensor_scalar(out=nw[:, s], in0=w2[:, s], scalar1=-1.0, scalar2=0.0, op0=ALU.mult, op1=ALU.add)
             nc.gpsimd.tensor_scalar(
@@ -245,141 +253,12 @@ def tile_modernncastochasticneighbourregressor_x1_kernel(tc, q, c, g, h, y, u, r
             nc.scalar.activation(out=x[i][:], in_=x[i][:], func=ACT.Sqrt, scale=rk[:, i : i + 1])
 
         def y_group(a):
-            nc.vector.tensor_copy(
-                out=yg[:, a, :].rearrange("p (t c j) -> p t c j", t=4, j=4),
-                in_=yraw[:, a, :, :].rearrange("p j (c t) -> p t c j", t=4),
-            )
+            out = yg[:, a, :].rearrange("p (t c j) -> p t c j", t=4, j=4)
+            in_ = yraw[:, a, :, :].rearrange("p j (c t) -> p t c j", t=4)
+            nc.scalar.copy(out=out, in_=in_)
 
         def y_quant(a):
             nc.vector.quantize_mx(out=y_codes[:, a, :].bitcast(FP8X4), scales=y_scales[:, a, :], in_=yg[:, a, :])
-
-        ub = {}
-
-        def spread(a):
-            ub[a] = mm.tile([P, 512], F32, name="bank")
-            nc.tensor.matmul(ub[a][:], lhsT=ones[:], rhs=rows[:, 512 * a : 512 * a + 512], start=True, stop=True)
-
-        def far(a):
-            nc.vector.tensor_scalar(
-                out=big[:, 512 * a : 512 * a + 512].rearrange("p (v c e) -> p v c e", v=2, e=2),
-                in0=ub[a][:].rearrange("p (c v e) -> p v c e", v=2, e=2),
-                scalar1=0.7,
-                scalar2=FAR,
-                op0=ALU.is_ge,
-                op1=ALU.mult,
-            )
-
-        def gain(a):
-            nc.scalar.copy(
-                out=r_b[:, 512 * a : 512 * a + 512].rearrange("p (v c e) -> p v c e", v=2, e=2),
-                in_=ub[2 + a][:].rearrange("p (c v e) -> p v c e", v=2, e=2),
-            )
-
-        order = [(0, 0), (0, 1), (1, 0), (1, 1)]
-        spread(0)
-        spread(1)
-        for k in range(4):
-            c_turn(*order[k])
-        far(0)
-        far(1)
-        for k in range(4):
-            c_scale(*order[k])
-            c_square(*order[k])
-            if k:
-                c_quant(*order[k - 1])
-        q_turn(0)
-        q_turn(1)
-        c_sum(0)
-        q_scale(0)
-        c_quant(1, 1)
-        q_square(0)
-        q_turn(2)
-        q_scale(1)
-        q_quant(0)
-        q_square(1)
-        c_mask(0)
-        q_quant(1)
-        cross(0, 0)
-        cross(1, 0)
-        cross(2, 0)
-        c_sum(1)
-        q_scale(2)
-        q_square(2)
-        add_c2(0, 0)
-        q_quant(2)
-        add_c2(1, 0)
-        cross(3, 0)
-        q_turn(3)
-        q_sum(0)
-        q_keep(0)
-        add_c2(2, 0)
-        add_c2(3, 0)
-        q_scale(3)
-        q_square(3)
-        c_mask(1)
-        q_quant(3)
-        cross(0, 1)
-        cross(1, 1)
-        q_turn(4)
-
-        NP = NT // 2
-        for i in range(NT):
-            if i < 4:
-                if i + 2 < 4:
-                    cross(i + 2, 1)
-                add_c2(i, 1)
-            else:
-                add_c2(i, 0)
-                add_c2(i, 1)
-            if 2 <= i < NT - 2:
-                cross(i + 2, 0)
-                cross(i + 2, 1)
-            if i % 2 == 0 and 1 + i // 2 < NP:
-                q_sum(1 + i // 2)
-            if i:
-                add_q2(i - 1)
-            j = 4 + i // 2
-            if i % 2 == 0 and j < NP:
-                q_scale(j)
-                q_square(j)
-            if i % 2 == 1 and j < NP:
-                q_quant(j)
-                if j + 1 < NP:
-                    q_turn(j + 1)
-            if i % 2 == 0 and 1 + i // 2 < NP:
-                q_keep(1 + i // 2)
-            if i % 2 == 0 and i:
-                s = slice(i - 2, i)
-                row_a(s)
-            if i % 2 == 1 and i > 1:
-                s = slice(i - 3, i - 1)
-                row_b(s)
-                row_c(s)
-                root(i - 3)
-                root(i - 2)
-            if i == 9:
-                spread(2)
-                gain(0)
-                spread(3)
-                gain(1)
-        row_a(slice(NT - 2, NT - 1))
-        add_q2(NT - 1)
-        row_b(slice(NT - 2, NT - 1))
-        row_c(slice(NT - 2, NT - 1))
-        root(NT - 2)
-        row_a(slice(NT - 1, NT))
-        y_group(0)
-        row_b(slice(NT - 1, NT))
-        row_c(slice(NT - 1, NT))
-        root(NT - 1)
-        y_group(1)
-        y_quant(0)
-        y_quant(1)
-
-        ars, arts, outs = {}, {}, {}
-        art_codes, art_scales = {}, {}
-        ocs = {}
-        ogs = {}
 
         def expo(i):
             nc.scalar.activation(
@@ -395,48 +274,42 @@ def tile_modernncastochasticneighbourregressor_x1_kernel(tc, q, c, g, h, y, u, r
             nc.vector.reciprocal(out=rs[:, i : i + 1], in_=ssum[:, i : i + 1])
 
         def weigh(i):
-            t = work.tile([P, N], BF16, name="ar", align_bytes=64)
-            ars[i] = t
-            nc.vector.scalar_tensor_tensor(
-                out=t[:], in0=x[i][:], scalar=rs[:, i : i + 1], in1=r_b[:], op0=ALU.mult, op1=ALU.mult
-            )
+            if i in SCALE_V:
+                nc.vector.tensor_scalar(out=x[i][:], in0=x[i][:], scalar1=rs[:, i : i + 1], scalar2=None, op0=ALU.mult)
+            else:
+                for n in range(1):
+                    s = slice(1024 * n, 1024 * (n + 1))
+                    nc.gpsimd.tensor_scalar(
+                        out=x[i][:, s], in0=x[i][:, s], scalar1=rs[:, i : i + 1], scalar2=1.0, op0=ALU.mult, op1=ALU.mult
+                    )
 
-        def turn(i):
-            t = mm.tile([P, 512], F32, name="bank")
-            trs["a", i] = t
-            words = ars[i][:].bitcast(F32)
+        def turn(i, n):
+            t = bank("x", "a", i, n)
             for k in range(4):
-                nc.tensor.transpose(t[:, P * k : P * k + P], words[:, P * k : P * k + P], ident[:])
+                s = 512 * n + P * k
+                nc.tensor.transpose(t[:, P * k : P * k + P], x[i][:, s : s + P], ident[:])
 
         def unpack(i):
             t = work.tile([P, 1024], BF16, name="art", align_bytes=64)
-            arts[i] = t
-            nc.vector.tensor_copy(
-                out=t[:].bitcast(F32).rearrange("p (a b v) -> p a b v", a=2, v=2),
-                in_=trs["a", i][:].rearrange("p (a v b) -> p a b v", a=2, v=2),
-            )
+            tiles["art", i] = t
+            for n in range(2):
+                nc.vector.tensor_tensor(
+                    out=t[:, 512 * n : 512 * n + 512].rearrange("p (b t) -> p b t", t=4),
+                    in0=tiles["a", i, n][:].rearrange("p (t b) -> p b t", t=4),
+                    in1=r8[:, n, :].unsqueeze(1).to_broadcast([P, P, 4]),
+                    op=ALU.mult,
+                )
 
         def a_quant(i):
             k = work.tile([P, 256], U32, name="art_codes", align_bytes=64)
             s = work.tile([P, 256], U8, name="art_scales", align_bytes=64)
-            art_codes[i], art_scales[i] = k, s
-            nc.vector.quantize_mx(out=k[:].bitcast(FP8X4), scales=s[:], in_=arts[i][:])
+            tiles["codes", i], tiles["scales", i] = k, s
+            nc.vector.quantize_mx(out=k[:].bitcast(FP8X4), scales=s[:], in_=tiles["art", i][:])
 
         def second(i):
-            t = mm.tile([P, 512], F32, name="bank")
-            tt = mm.tile([P, 512], F32, name="bank")
-            outs[i] = (t, tt)
-            k, s = art_codes[i], art_scales[i]
-            for a in range(2):
-                nc.tensor.matmul_mx(
-                    out=t[:],
-                    lhsT=k[:, P * a : P * a + P].bitcast(FP8X4),
-                    lhsT_scale=s[:, P * a : P * a + P],
-                    rhs=y_codes[:, a, :].bitcast(FP8X4),
-                    rhs_scale=y_scales[:, a, :],
-                    start=(a == 0),
-                    stop=(a == 1),
-                )
+            tt = bank("o", "ot", i)
+            t = bank("o", "o", i)
+            k, s = tiles["codes", i], tiles["scales", i]
             for m in range(4):
                 for a in range(2):
                     nc.tensor.matmul_mx(
@@ -448,27 +321,37 @@ def tile_modernncastochasticneighbourregressor_x1_kernel(tc, q, c, g, h, y, u, r
                         start=(a == 0),
                         stop=(a == 1),
                     )
+            for a in range(2):
+                nc.tensor.matmul_mx(
+                    out=t[:],
+                    lhsT=k[:, P * a : P * a + P].bitcast(FP8X4),
+                    lhsT_scale=s[:, P * a : P * a + P],
+                    rhs=y_codes[:, a, :].bitcast(FP8X4),
+                    rhs_scale=y_scales[:, a, :],
+                    start=(a == 0),
+                    stop=(a == 1),
+                )
 
         def leave(i):
             t = work.tile([P, C], F32, name="o")
-            nc.scalar.copy(
-                out=t[:].rearrange("p (c m) -> p c m", m=4), in_=outs[i][0][:].rearrange("p (m c) -> p c m", m=4)
-            )
+            copy = nc.vector.tensor_copy if i in LEAVE_V else nc.scalar.copy
+            copy(out=t[:].rearrange("p (c m) -> p c m", m=4), in_=tiles["o", i][:].rearrange("p (m c) -> p c m", m=4))
             nc.sync.dma_start(out=out_0[P * i : P * i + P, :], in_=t[:])
 
         def leave_t(i):
             if i % 2 == 0:
                 og = work.tile([P, 1024], BF16, name="og", align_bytes=64)
-                ogs[i // 2] = og
-            nc.scalar.copy(
-                out=ogs[i // 2][:, 512 * (i % 2) : 512 * (i % 2) + 512].rearrange("p (b m) -> p b m", m=4),
-                in_=outs[i][1][:].rearrange("p (m b) -> p b m", m=4),
+                tiles["og", i // 2] = og
+            copy = nc.vector.tensor_copy if i in LEAVE_T_V else nc.scalar.copy
+            copy(
+                out=tiles["og", i // 2][:, 512 * (i % 2) : 512 * (i % 2) + 512].rearrange("p (b m) -> p b m", m=4),
+                in_=tiles["ot", i][:].rearrange("p (m b) -> p b m", m=4),
             )
 
         def o_quant(j):
             k = work.tile([P, 256], U32, name="o_codes", align_bytes=64)
             s = slice(256 * j, 256 * j + 256)
-            nc.vector.quantize_mx(out=k[:].bitcast(FP8X4), scales=o_scales[:, s], in_=ogs[j][:])
+            nc.vector.quantize_mx(out=k[:].bitcast(FP8X4), scales=o_scales[:, s], in_=tiles["og", j][:])
             nc.sync.dma_start(
                 out=out_1[0, :, s, :].rearrange("p m t -> p (m t)").bitcast(I32), in_=k[:].bitcast(I32)
             )
@@ -479,22 +362,115 @@ def tile_modernncastochasticneighbourregressor_x1_kernel(tc, q, c, g, h, y, u, r
                         out=out_2[0, 4 * b : 4 * b + 4, s].bitcast(I32), in_=o_scales[32 * b : 32 * b + 4, s].bitcast(I32)
                     )
 
-        expo(0)
-        for i in range(NT + 4):
+        for k in range(4):
+            c_turn(k)
+            c_scale(k)
+            c_square(k)
+            if k:
+                c_quant(k - 1)
+        q_turn(0)
+        c_col(0)
+        c_col(1)
+        c_add(0)
+        q_scale(0)
+        c_quant(3)
+        q_square(0)
+        q_turn(1)
+        c_bcast(0)
+        c_keep(0)
+        q_quant(0)
+        q_scale(1)
+        c_col(2)
+        c_col(3)
+        c_add(1)
+        q_square(1)
+        q_turn(2)
+        c_bcast(1)
+        cross(0, 0)
+        q_quant(1)
+        q_scale(2)
+        q_square(2)
+        c_keep(1)
+        cross(0, 1)
+        q_sum(0)
+        y_group(0)
+        q_keep(0)
+        q_turn(3)
+        q_quant(2)
+
+
+        D = 14
+
+        def stage(i):
+            dist(i, 0)
+            dist(i, 1)
+            if i > 1:
+                row_b(i - 2)
+            if i > 0 and i % 2 == 0 and i // 2 < NP:
+                q_keep(i // 2)
             if i + 1 < NT:
-                expo(i + 1)
-            if i < NT:
-                inv(i)
-            if 3 <= i <= NT + 2:
-                leave(i - 3)
-                leave_t(i - 3)
-            if 2 <= i <= NT + 1:
-                a_quant(i - 2)
-                second(i - 2)
-            if i < NT:
-                weigh(i)
-                turn(i)
-            if i >= 4 and i % 2 == 0:
-                o_quant((i - 4) // 2)
-            if 1 <= i <= NT:
-                unpack(i - 1)
+                cross(i + 1, 0)
+                cross(i + 1, 1)
+            if i % 2 == 0 and 3 + i // 2 < NP:
+                q_scale(3 + i // 2)
+                q_square(3 + i // 2)
+            if i % 2 == 1 and 1 + i // 2 < NP:
+                q_sum(1 + i // 2)
+            if i:
+                low(i - 1)
+                row_a(i - 1)
+            if i % 2 == 1 and 3 + i // 2 < NP:
+                q_quant(3 + i // 2)
+                if 4 + i // 2 < NP:
+                    q_turn(4 + i // 2)
+
+        exps = list(range(NT))
+        invs = list(range(NT))
+        for s in range(NT + D + 3):
+            t = s - D
+            if 1 <= t <= NT:
+                a_quant(t - 1)
+                second(t - 1)
+            if 0 <= t + 1 < NT:
+                turn(t + 1, 0)
+            if s < NT:
+                stage(s)
+            if s == NT:
+                row_b(NT - 2)
+                low(NT - 1)
+                row_a(NT - 1)
+            if s == NT + 1:
+                row_b(NT - 1)
+            if 0 <= t < NT:
+                unpack(t)
+            if 0 <= t + 1 < NT:
+                turn(t + 1, 1)
+            if s == 1:
+                y_group(1)
+            if s == NT - 6:
+                y_quant(0)
+            if s == NT - 5:
+                y_quant(1)
+            if t >= 4 and t % 2 == 0 and (t - 4) // 2 < NP:
+                o_quant((t - 4) // 2)
+            if 2 <= s < NT + 2:
+                root(s - 2)
+            if s == 9:
+                row_c(0, H)
+            if s == 17:
+                row_c(H, NT - H)
+            if 9 <= s < 17:
+                for k in range(8):
+                    if exps and exps[0] < H:
+                        expo(exps.pop(0))
+            if s >= 17 and exps:
+                expo(exps.pop(0))
+            k = t - 1
+            if 0 <= k < NT:
+                leave_t(k)
+                leave(k)
+            for k in range(2):
+                if invs and invs[0] < H and s >= 11 or invs and invs[0] >= H and s >= 18 and k == 0:
+                    kk = invs.pop(0)
+                    inv(kk)
+                    weigh(kk)

@@ -18,14 +18,16 @@ NT = B // P
 NP = NT // 2
 FLOPS = 2 * B * N * E + 2 * B * N * C
 
+UNPACK_FIRST = [1,1,0,1,1,1,1,1,1,0,0,1,1,1,1,1]
+OG_FIRST = [1,2,5,7,8,10,12,14]
 FAR = 2.5e17
 TINY = 1e-12
 SPOT = 1.5
 H = 8
-LEAVE_V = [6,8,10]
-LEAVE_T_V = []
-SCALE_V = []
-KEEP_S = False
+LEAVE_V = [0,1,2,13]
+LEAVE_T_V = [0,1,2,3,13,14]
+SCALE_V = [14]
+KEEP_S = [1]
 
 
 def tile_modernncastochasticneighbourregressor_x1_kernel(tc, q, c, g, h, y, u, r, out_0, out_1, out_2):
@@ -35,15 +37,12 @@ def tile_modernncastochasticneighbourregressor_x1_kernel(tc, q, c, g, h, y, u, r
         xs = ctx.enter_context(tc.tile_pool(name="xs", bufs=NT))
         work = ctx.enter_context(tc.tile_pool(name="work", bufs=3))
         mm = ctx.enter_context(tc.psum_pool(name="mm", bufs=2))
-        qp = ctx.enter_context(tc.psum_pool(name="qp", bufs=1))
 
         ident = keep.tile([P, P], F32, name="ident")
         g4 = keep.tile([P, 4], BF16, name="g4")
         h4 = keep.tile([P, 4], BF16, name="h4")
         gh = keep.tile([P, 4], F32, name="gh")
-        u8 = keep.tile([P, 2, 4], BF16, name="u8")
         r8 = keep.tile([P, 2, 4], BF16, name="r8")
-        far = keep.tile([P, 8], F32, name="far")
         craw = keep.tile([P, 2, 4, E], BF16, name="craw")
         yraw = keep.tile([P, 2, 4, C], BF16, name="yraw")
         qraw = keep.tile([P, NT, E], BF16, name="qraw")
@@ -56,9 +55,14 @@ def tile_modernncastochasticneighbourregressor_x1_kernel(tc, q, c, g, h, y, u, r
         y_codes = keep.tile([P, 2, C], U32, name="y_codes", align_bytes=64)
         y_scales = keep.tile([P, 2, C], U8, name="y_scales", align_bytes=64)
         o_scales = keep.tile([P, B], U8, name="o_scales", align_bytes=64)
-        sums = qp.tile([P, NT + 8], F32, name="sums")
         q2 = keep.tile([P, NT], F32, name="q2")
-        c2 = keep.tile([P, 8], F32, name="c2")
+        rows = keep.tile([P, 2 * E], BF16, name="rows")
+        ones = keep.tile([P, P], BF16, name="ones")
+        ones32 = keep.tile([P, P], F32, name="ones32")
+        urow = keep.tile([1, N], BF16, name="urow")
+        farrow = keep.tile([P, N], F32, name="farrow")
+        g_b = keep.tile([P, E], F32, name="g_b")
+        gh_b = keep.tile([P, E], F32, name="gh_b")
         xmin = keep.tile([P, NT], F32, name="xmin")
         xm = keep.tile([P, NT], F32, name="xm")
         rk = keep.tile([P, NT], F32, name="rk")
@@ -71,11 +75,17 @@ def tile_modernncastochasticneighbourregressor_x1_kernel(tc, q, c, g, h, y, u, r
 
         ctx.enter_context(tc.manual_schedule())
 
+        make_identity(nc, ident[:])
+        nc.vector.memset(rows[:].bitcast(I32), 0)
+        nc.vector.memset(ones[:], 1.0)
+        nc.vector.memset(ones32[:], 1.0)
+        nc.gpsimd.memset(farrow[:], 0.0)
+        nc.scalar.dma_start(out=rows[0:1, 0:E], in_=g.unsqueeze(0))
+        nc.scalar.dma_start(out=rows[0:1, E : 2 * E], in_=h.unsqueeze(0))
         nc.scalar.dma_start(out=h4[:], in_=h.rearrange("(p t) -> p t", t=4))
         nc.scalar.dma_start(out=g4[:], in_=g.rearrange("(p t) -> p t", t=4))
-        nc.scalar.dma_start(out=u8[:], in_=u.rearrange("(a p t) -> p a t", a=2, t=4))
+        nc.scalar.dma_start(out=urow[:], in_=u.unsqueeze(0))
         nc.scalar.dma_start(out=r8[:], in_=r.rearrange("(a p t) -> p a t", a=2, t=4))
-        make_identity(nc, ident[:])
         c_view = c.rearrange("(a p t) d -> a p t d", a=2, t=4)
         q_view = q.rearrange("(k p) d -> p k d", p=P)
         y_view = y.rearrange("(a p t) d -> a p t d", a=2, t=4)
@@ -89,8 +99,8 @@ def tile_modernncastochasticneighbourregressor_x1_kernel(tc, q, c, g, h, y, u, r
                     nc.sync.dma_start(out=yraw[:, a, :, :], in_=y_view[a])
         nc.vector.tensor_tensor(out=gh[:], in0=g4[:], in1=h4[:], op=ALU.mult)
         nc.vector.tensor_scalar(
-            out=far[:],
-            in0=u8[:].rearrange("p a t -> p (a t)"),
+            out=farrow[0:1, :].rearrange("p (a t c) -> p a t c", a=2, t=4),
+            in0=urow[:].rearrange("p (a c t) -> p a t c", a=2, t=4),
             scalar1=0.7,
             scalar2=FAR,
             op0=ALU.is_ge,
@@ -99,7 +109,7 @@ def tile_modernncastochasticneighbourregressor_x1_kernel(tc, q, c, g, h, y, u, r
 
         tiles = {}
 
-        depth = {"x": 3, "o": 4}
+        depth = {"x": 4, "o": 4}
 
         def bank(tag, *key):
             t = mm.tile([P, 512], F32, name=tag, bufs=depth[tag])
@@ -126,24 +136,6 @@ def tile_modernncastochasticneighbourregressor_x1_kernel(tc, q, c, g, h, y, u, r
                 op=ALU.mult,
             )
 
-        def square_rows(key):
-            b16 = tiles[key][:].bitcast(BF16).rearrange("p (w r d) -> p w r d", w=2, d=2)
-            t = work.tile([P, 4, 256], F32, name="sq", bufs=6)
-            tiles["sq", key] = t
-            for d in range(2):
-                nc.scalar.activation(out=t[:, d:4:2, :], in_=b16[:, :, :, d], func=ACT.Square)
-
-        def sum_rows(key, first):
-            for k in range(2):
-                for s in range(4):
-                    nc.tensor.matmul(
-                        sums[:, first + k : first + k + 1],
-                        lhsT=tiles["sq", key][:, s, k * P : k * P + P],
-                        rhs=gh[:, s : s + 1],
-                        start=(s == 0),
-                        stop=(s == 3),
-                    )
-
         def quantise(codes, scales, key, j):
             s = slice(256 * j, 256 * j + 256)
             nc.vector.quantize_mx(out=codes[:, s].bitcast(FP8X4), scales=scales[:, s], in_=tiles["grp", key][:])
@@ -154,32 +146,44 @@ def tile_modernncastochasticneighbourregressor_x1_kernel(tc, q, c, g, h, y, u, r
         def c_scale(k):
             scale_rows(("c", k), h4)
 
+        def gb(i):
+            for k in range(2):
+                t = head_bank("gb", k)
+                nc.tensor.matmul(t[:], lhsT=ones[:], rhs=rows[:, E * k : E * k + E], start=True, stop=True)
+
+        def g_keep(i):
+            nc.scalar.copy(out=g_b[:], in_=tiles["gb", 0][:])
+
+        def gh_mul(i):
+            nc.vector.tensor_tensor(out=gh_b[:], in0=tiles["gb", 1][:], in1=g_b[:], op=ALU.mult)
+
         def c_square(k):
-            square_rows(("c", k))
+            b16 = tiles["c", k][:].bitcast(BF16).rearrange("p (w r d) -> p w r d", w=2, d=2)
+            t = work.tile([P, 4, 256], F32, name="sq", bufs=4)
+            tiles["sq", k] = t
+            for d in range(2):
+                nc.scalar.activation(out=t[:, d:4:2, :], in_=b16[:, :, :, d], func=ACT.Square)
 
         def c_quant(k):
             quantise(ch_codes, ch_scales, ("c", k), k)
 
-        def c_col(k):
-            sum_rows(("c", k), NT + 2 * k)
-
-        def c_add(a):
-            s = slice(4 * a, 4 * a + 4)
-            nc.vector.tensor_tensor(out=c2[:, s], in0=sums[:, NT + 4 * a : NT + 4 * a + 4], in1=far[:, s], op=ALU.add)
-
-        def c_bcast(a):
-            t = bank("x", "c2", a)
-            for k in range(4):
+        def c_sum(k):
+            if ("c2", k // 2) not in tiles:
+                bank("x", "c2", k // 2)
+            s = slice(256 * (k % 2), 256 * (k % 2) + 256)
+            t = tiles["c2", k // 2]
+            nc.tensor.matmul(t[:, s], lhsT=ones32[:], rhs=farrow[:, 256 * k : 256 * k + 256], start=True, stop=False)
+            for m in range(4):
                 nc.tensor.matmul(
-                    t[:, P * k : P * k + P],
-                    lhsT=c2[:, 4 * a + k : 4 * a + k + 1].to_broadcast([P, P]),
-                    rhs=ident[:],
-                    start=True,
-                    stop=True,
+                    t[:, s],
+                    lhsT=gh[:, m : m + 1].to_broadcast([P, P]),
+                    rhs=tiles["sq", k][:, m, :],
+                    start=False,
+                    stop=(m == 3),
                 )
 
         def c_keep(a):
-            copy = nc.scalar.copy if KEEP_S else nc.vector.tensor_copy
+            copy = nc.scalar.copy if a in KEEP_S else nc.vector.tensor_copy
             copy(out=c2m[:, 512 * a : 512 * a + 512], in_=tiles["c2", a][:])
 
         def q_turn(j):
@@ -188,17 +192,18 @@ def tile_modernncastochasticneighbourregressor_x1_kernel(tc, q, c, g, h, y, u, r
         def q_scale(j):
             scale_rows(("q", j), g4)
 
-        def q_square(j):
-            square_rows(("q", j))
-
         def q_quant(j):
             quantise(q_codes, q_scales, ("q", j), j)
 
-        def q_sum(j):
-            sum_rows(("q", j), 2 * j)
+        def q_w(i):
+            t = work.tile([P, E], F32, name="qw")
+            tiles["qw", i] = t
+            nc.gpsimd.tensor_tensor(out=t[:], in0=qraw[:, i, :], in1=gh_b[:], op=ALU.mult)
+            nc.gpsimd.tensor_tensor(out=t[:], in0=t[:], in1=qraw[:, i, :], op=ALU.mult)
 
-        def q_keep(j):
-            nc.vector.tensor_copy(out=q2[:, 2 * j : 2 * j + 2], in_=sums[:, 2 * j : 2 * j + 2])
+        def q_acc(i):
+            t = tiles["qw", i]
+            nc.scalar.activation(out=t[:], in_=t[:], func=ACT.Copy, accum_out=q2[:, i : i + 1])
 
         def cross(i, n):
             t = bank("x", "cross", i, n)
@@ -241,8 +246,8 @@ def tile_modernncastochasticneighbourregressor_x1_kernel(tc, q, c, g, h, y, u, r
             s = slice(i, i + 1)
             nc.vector.reciprocal(out=rk[:, s], in_=xm[:, s])
 
-        def row_c(i, m):
-            s = slice(i, i + m)
+        def row_c(i):
+            s = slice(0, H) if i == 0 else slice(H, NT)
             nc.scalar.activation(out=w2[:, s], in_=xm[:, s], func=ACT.Sqrt, scale=4.0)
             nc.gpsimd.tensor_scalar(out=nw[:, s], in0=w2[:, s], scalar1=-1.0, scalar2=0.0, op0=ALU.mult, op1=ALU.add)
             nc.gpsimd.tensor_scalar(
@@ -289,16 +294,16 @@ def tile_modernncastochasticneighbourregressor_x1_kernel(tc, q, c, g, h, y, u, r
                 s = 512 * n + P * k
                 nc.tensor.transpose(t[:, P * k : P * k + P], x[i][:, s : s + P], ident[:])
 
-        def unpack(i):
-            t = work.tile([P, 1024], BF16, name="art", align_bytes=64)
-            tiles["art", i] = t
-            for n in range(2):
-                nc.vector.tensor_tensor(
-                    out=t[:, 512 * n : 512 * n + 512].rearrange("p (b t) -> p b t", t=4),
-                    in0=tiles["a", i, n][:].rearrange("p (t b) -> p b t", t=4),
-                    in1=r8[:, n, :].unsqueeze(1).to_broadcast([P, P, 4]),
-                    op=ALU.mult,
-                )
+        def unpack(i, n):
+            if n == UNPACK_FIRST[i]:
+                t = work.tile([P, 1024], BF16, name="art", bufs=6, align_bytes=64)
+                tiles["art", i] = t
+            nc.vector.tensor_tensor(
+                out=tiles["art", i][:, 512 * n : 512 * n + 512].rearrange("p (b t) -> p b t", t=4),
+                in0=tiles["a", i, n][:].rearrange("p (t b) -> p b t", t=4),
+                in1=r8[:, n, :].unsqueeze(1).to_broadcast([P, P, 4]),
+                op=ALU.mult,
+            )
 
         def a_quant(i):
             k = work.tile([P, 256], U32, name="art_codes", align_bytes=64)
@@ -308,7 +313,6 @@ def tile_modernncastochasticneighbourregressor_x1_kernel(tc, q, c, g, h, y, u, r
 
         def second(i):
             tt = bank("o", "ot", i)
-            t = bank("o", "o", i)
             k, s = tiles["codes", i], tiles["scales", i]
             for m in range(4):
                 for a in range(2):
@@ -321,6 +325,10 @@ def tile_modernncastochasticneighbourregressor_x1_kernel(tc, q, c, g, h, y, u, r
                         start=(a == 0),
                         stop=(a == 1),
                     )
+
+        def third(i):
+            t = bank("o", "o", i)
+            k, s = tiles["codes", i], tiles["scales", i]
             for a in range(2):
                 nc.tensor.matmul_mx(
                     out=t[:],
@@ -333,14 +341,14 @@ def tile_modernncastochasticneighbourregressor_x1_kernel(tc, q, c, g, h, y, u, r
                 )
 
         def leave(i):
-            t = work.tile([P, C], F32, name="o")
+            t = work.tile([P, C], F32, name="o", bufs=6)
             copy = nc.vector.tensor_copy if i in LEAVE_V else nc.scalar.copy
             copy(out=t[:].rearrange("p (c m) -> p c m", m=4), in_=tiles["o", i][:].rearrange("p (m c) -> p c m", m=4))
             nc.sync.dma_start(out=out_0[P * i : P * i + P, :], in_=t[:])
 
         def leave_t(i):
-            if i % 2 == 0:
-                og = work.tile([P, 1024], BF16, name="og", align_bytes=64)
+            if i == OG_FIRST[i // 2]:
+                og = work.tile([P, 1024], BF16, name="og", bufs=8, align_bytes=64)
                 tiles["og", i // 2] = og
             copy = nc.vector.tensor_copy if i in LEAVE_T_V else nc.scalar.copy
             copy(
@@ -348,129 +356,212 @@ def tile_modernncastochasticneighbourregressor_x1_kernel(tc, q, c, g, h, y, u, r
                 in_=tiles["ot", i][:].rearrange("p (m b) -> p b m", m=4),
             )
 
+        stored = []
+
         def o_quant(j):
-            k = work.tile([P, 256], U32, name="o_codes", align_bytes=64)
+            k = work.tile([P, 256], U32, name="o_codes", bufs=8, align_bytes=64)
             s = slice(256 * j, 256 * j + 256)
             nc.vector.quantize_mx(out=k[:].bitcast(FP8X4), scales=o_scales[:, s], in_=tiles["og", j][:])
             nc.sync.dma_start(
                 out=out_1[0, :, s, :].rearrange("p m t -> p (m t)").bitcast(I32), in_=k[:].bitcast(I32)
             )
-            if j % 4 == 3:
-                s = slice(256 * (j - 3), 256 * j + 256)
+            stored.append(j)
+            half = [k for k in stored if k // 4 == j // 4]
+            if len(half) == 4:
+                s = slice(1024 * (j // 4), 1024 * (j // 4) + 1024)
                 for b in range(4):
                     nc.sync.dma_start(
                         out=out_2[0, 4 * b : 4 * b + 4, s].bitcast(I32), in_=o_scales[32 * b : 32 * b + 4, s].bitcast(I32)
                     )
 
-        for k in range(4):
-            c_turn(k)
-            c_scale(k)
-            c_square(k)
-            if k:
-                c_quant(k - 1)
-        q_turn(0)
-        c_col(0)
-        c_col(1)
-        c_add(0)
-        q_scale(0)
-        c_quant(3)
-        q_square(0)
-        q_turn(1)
-        c_bcast(0)
-        c_keep(0)
-        q_quant(0)
-        q_scale(1)
-        c_col(2)
-        c_col(3)
-        c_add(1)
-        q_square(1)
-        q_turn(2)
-        c_bcast(1)
-        cross(0, 0)
-        q_quant(1)
-        q_scale(2)
-        q_square(2)
-        c_keep(1)
-        cross(0, 1)
-        q_sum(0)
-        y_group(0)
-        q_keep(0)
-        q_turn(3)
-        q_quant(2)
+        fns = {
+            "gb": gb, "g_keep": g_keep, "gh_mul": gh_mul, "c_turn": c_turn, "c_scale": c_scale, "c_square": c_square, "c_quant": c_quant,
+            "c_sum": c_sum, "c_keep": c_keep, "q_turn": q_turn, "q_scale": q_scale, "q_quant": q_quant, "q_w": q_w, "q_acc": q_acc,
+            "cross": cross, "dist": dist, "low": low, "row_a": row_a, "row_b": row_b, "row_c": row_c, "root": root, "y_group": y_group,
+            "y_quant": y_quant, "expo": expo, "inv": inv, "weigh": weigh, "turn": turn, "unpack": unpack, "a_quant": a_quant,
+            "second": second, "third": third, "leave": leave, "leave_t": leave_t, "o_quant": o_quant,
+        }
 
+        def reads(f, i, n):
+            if f in ("g_keep",):
+                return [("gb", 0, 0)]
+            if f == "gh_mul":
+                return [("g_keep", 0, 0)]
+            if f in ("c_scale", "c_square"):
+                return [("c_turn", i, 0)]
+            if f == "c_quant":
+                return [("c_scale", i, 0)]
+            if f == "c_sum":
+                return [("c_square", i, 0)]
+            if f == "c_keep":
+                return [("c_sum", 2 * i, 0), ("c_sum", 2 * i + 1, 0)]
+            if f == "q_scale":
+                return [("q_turn", i, 0)]
+            if f == "q_quant":
+                return [("q_scale", i, 0)]
+            if f == "q_w":
+                return [("gh_mul", 0, 0)]
+            if f == "q_acc":
+                return [("q_w", i, 0)]
+            if f == "cross":
+                return [("q_quant", i // 2, 0), ("c_quant", 2 * n, 0), ("c_quant", 2 * n + 1, 0)]
+            if f == "dist":
+                return [("cross", i, n), ("c_keep", n, 0)]
+            if f == "low":
+                return [("dist", i, 0), ("dist", i, 1), ("q_acc", i, 0)]
+            if f == "row_a":
+                return [("low", i, 0)]
+            if f == "row_b":
+                return [("row_a", i, 0)]
+            if f == "row_c":
+                return [("row_a", k, 0) for k in (range(H) if i == 0 else range(H, NT))]
+            if f == "root":
+                return [("row_b", i, 0)]
+            if f == "y_quant":
+                return [("y_group", i, 0)]
+            if f == "expo":
+                return [("root", i, 0), ("row_c", 0 if i < H else 1, 0)]
+            if f == "inv":
+                return [("expo", i, 0)]
+            if f == "weigh":
+                return [("inv", i, 0)]
+            if f == "turn":
+                return [("weigh", i, 0)]
+            if f == "unpack":
+                return [("turn", i, n)]
+            if f == "a_quant":
+                return [("unpack", i, 0), ("unpack", i, 1)]
+            if f in ("second", "third"):
+                return [("a_quant", i, 0), ("y_quant", 0, 0), ("y_quant", 1, 0)]
+            if f == "leave":
+                return [("third", i, 0)]
+            if f == "leave_t":
+                first = OG_FIRST[i // 2]
+                return [("second", i, 0)] + ([] if i == first else [("leave_t", first, 0)])
+            if f == "o_quant":
+                return [("leave_t", 2 * i, 0), ("leave_t", 2 * i + 1, 0)]
+            return []
 
-        D = 14
+        def fills(f, i, n):
+            if f == "c_turn":
+                return [("o", [("c_scale", i, 0), ("c_square", i, 0)])]
+            if f == "gb":
+                return [("o", [("g_keep", 0, 0)]), ("o", [("gh_mul", 0, 0)])]
+            if f == "q_turn":
+                return [("o", [("q_scale", i, 0)])]
+            if f == "c_sum" and ("c_sum", i ^ 1, 0) not in done:
+                return [("x", [("c_keep", i // 2, 0)])]
+            if f == "cross":
+                return [("x", [("dist", i, n)])]
+            if f == "turn":
+                return [("x", [("unpack", i, n)])]
+            if f == "second":
+                return [("o", [("leave_t", i, 0)])]
+            if f == "third":
+                return [("o", [("leave", i, 0)])]
+            if f == "c_scale":
+                return [("grp", [("c_quant", i, 0)])]
+            if f == "q_scale":
+                return [("grp", [("q_quant", i, 0)])]
+            if f == "q_w":
+                return [("qw", [("q_acc", i, 0)])]
+            if f == "unpack" and n == UNPACK_FIRST[i]:
+                return [("art", [("a_quant", i, 0)])]
+            if f == "a_quant":
+                return [("codes", [("second", i, 0), ("third", i, 0)])]
+            if f == "leave_t" and i == OG_FIRST[i // 2]:
+                return [("og", [("o_quant", i // 2, 0)])]
+            return []
 
-        def stage(i):
-            dist(i, 0)
-            dist(i, 1)
-            if i > 1:
-                row_b(i - 2)
-            if i > 0 and i % 2 == 0 and i // 2 < NP:
-                q_keep(i // 2)
-            if i + 1 < NT:
-                cross(i + 1, 0)
-                cross(i + 1, 1)
-            if i % 2 == 0 and 3 + i // 2 < NP:
-                q_scale(3 + i // 2)
-                q_square(3 + i // 2)
-            if i % 2 == 1 and 1 + i // 2 < NP:
-                q_sum(1 + i // 2)
-            if i:
-                low(i - 1)
-                row_a(i - 1)
-            if i % 2 == 1 and 3 + i // 2 < NP:
-                q_quant(3 + i // 2)
-                if 4 + i // 2 < NP:
-                    q_turn(4 + i // 2)
-
-        exps = list(range(NT))
-        invs = list(range(NT))
-        for s in range(NT + D + 3):
-            t = s - D
-            if 1 <= t <= NT:
-                a_quant(t - 1)
-                second(t - 1)
-            if 0 <= t + 1 < NT:
-                turn(t + 1, 0)
-            if s < NT:
-                stage(s)
-            if s == NT:
-                row_b(NT - 2)
-                low(NT - 1)
-                row_a(NT - 1)
-            if s == NT + 1:
-                row_b(NT - 1)
-            if 0 <= t < NT:
-                unpack(t)
-            if 0 <= t + 1 < NT:
-                turn(t + 1, 1)
-            if s == 1:
-                y_group(1)
-            if s == NT - 6:
-                y_quant(0)
-            if s == NT - 5:
-                y_quant(1)
-            if t >= 4 and t % 2 == 0 and (t - 4) // 2 < NP:
-                o_quant((t - 4) // 2)
-            if 2 <= s < NT + 2:
-                root(s - 2)
-            if s == 9:
-                row_c(0, H)
-            if s == 17:
-                row_c(H, NT - H)
-            if 9 <= s < 17:
-                for k in range(8):
-                    if exps and exps[0] < H:
-                        expo(exps.pop(0))
-            if s >= 17 and exps:
-                expo(exps.pop(0))
-            k = t - 1
-            if 0 <= k < NT:
-                leave_t(k)
-                leave(k)
-            for k in range(2):
-                if invs and invs[0] < H and s >= 11 or invs and invs[0] >= H and s >= 18 and k == 0:
-                    kk = invs.pop(0)
-                    inv(kk)
-                    weigh(kk)
+        orders = [
+            "gb:0:0 c_turn:0:0 q_turn:0:0 q_turn:2:0 c_turn:1:0 c_sum:0:0 q_turn:1:0 c_turn:3:0 "
+            "c_turn:2:0 q_turn:3:0 c_sum:1:0 cross:0:0 cross:4:0 c_sum:3:0 c_sum:2:0 q_turn:4:0 "
+            "cross:2:1 cross:2:0 cross:0:1 cross:3:1 cross:6:1 q_turn:7:0 cross:4:1 cross:1:1 cross:3:0 "
+            "cross:6:0 cross:1:0 cross:5:0 cross:5:1 cross:7:0 q_turn:5:0 q_turn:6:0 cross:7:1 "
+            "cross:10:0 cross:8:0 cross:10:1 cross:9:1 cross:9:0 cross:11:1 cross:8:1 cross:12:0 "
+            "cross:12:1 cross:13:1 cross:11:0 cross:13:0 turn:0:1 cross:15:1 cross:14:1 turn:0:0 "
+            "turn:1:1 cross:15:0 turn:1:0 cross:14:0 turn:5:1 turn:2:0 turn:2:1 third:0:0 second:0:0 "
+            "turn:3:1 turn:3:0 second:1:0 turn:5:0 turn:4:0 third:1:0 turn:4:1 turn:7:0 turn:7:1 "
+            "second:2:0 second:3:0 second:5:0 third:3:0 third:2:0 turn:6:1 turn:6:0 third:5:0 "
+            "second:4:0 third:4:0 turn:9:0 turn:8:1 turn:8:0 turn:10:0 third:7:0 second:7:0 turn:10:1 "
+            "turn:9:1 third:6:0 turn:11:1 turn:13:1 turn:11:0 second:6:0 second:10:0 turn:13:0 "
+            "turn:12:0 turn:12:1 second:8:0 third:10:0 third:8:0 turn:14:1 turn:15:1 turn:15:0 "
+            "turn:14:0 second:9:0 third:11:0 second:11:0 third:9:0 second:12:0 third:12:0 second:14:0 "
+            "second:13:0 third:14:0 second:15:0 third:13:0 third:15:0 ",
+            "gh_mul:0:0 q_scale:0:0 c_scale:0:0 c_scale:1:0 c_quant:0:0 q_quant:0:0 q_scale:2:0 "
+            "q_quant:2:0 q_scale:1:0 q_quant:1:0 c_quant:1:0 q_scale:3:0 c_keep:0:0 dist:0:0 dist:4:0 "
+            "q_quant:3:0 c_scale:2:0 y_quant:1:0 c_scale:3:0 c_quant:2:0 c_quant:3:0 q_scale:4:0 "
+            "dist:2:1 dist:2:0 dist:3:1 dist:0:1 dist:6:1 low:0:0 dist:4:1 low:2:0 low:4:0 row_b:2:0 "
+            "dist:1:1 dist:6:0 dist:3:0 dist:1:0 low:3:0 low:1:0 row_b:4:0 dist:5:1 q_quant:4:0 "
+            "row_b:3:0 q_scale:5:0 row_b:1:0 row_b:0:0 low:6:0 dist:7:1 dist:7:0 dist:5:0 row_b:6:0 "
+            "q_quant:5:0 low:7:0 low:5:0 row_b:7:0 dist:10:1 dist:10:0 dist:8:0 row_b:5:0 low:10:0 "
+            "q_scale:6:0 dist:8:1 dist:9:1 q_quant:6:0 q_scale:7:0 dist:11:1 dist:9:0 dist:12:0 "
+            "q_quant:7:0 low:9:0 inv:5:0 inv:1:0 dist:11:0 dist:13:0 dist:13:1 inv:0:0 low:8:0 "
+            "row_b:10:0 dist:12:1 low:13:0 low:11:0 row_b:8:0 unpack:0:1 dist:15:1 inv:3:0 inv:4:0 "
+            "row_b:9:0 inv:2:0 dist:14:1 low:12:0 unpack:1:1 row_b:11:0 row_b:13:0 unpack:0:0 dist:15:0 "
+            "a_quant:0:0 inv:7:0 y_quant:0:0 row_b:12:0 unpack:1:0 inv:6:0 dist:14:0 low:15:0 "
+            "unpack:5:1 low:14:0 unpack:2:0 row_b:15:0 a_quant:1:0 unpack:3:1 row_b:14:0 unpack:2:1 "
+            "unpack:3:0 leave:0:0 a_quant:2:0 unpack:5:0 a_quant:3:0 leave_t:1:0 leave_t:0:0 unpack:4:1 "
+            "a_quant:5:0 leave:1:0 inv:8:0 leave_t:2:0 unpack:4:0 inv:9:0 leave_t:3:0 unpack:7:1 "
+            "a_quant:4:0 inv:10:0 unpack:7:0 unpack:6:1 unpack:6:0 leave:2:0 a_quant:7:0 inv:11:0 "
+            "a_quant:6:0 inv:13:0 unpack:9:0 unpack:8:1 unpack:10:0 unpack:8:0 inv:12:0 unpack:10:1 "
+            "a_quant:8:0 unpack:9:1 a_quant:10:0 unpack:11:1 inv:14:0 unpack:13:1 weigh:14:0 inv:15:0 "
+            "unpack:11:0 unpack:13:0 unpack:12:1 unpack:12:0 o_quant:3:0 a_quant:11:0 a_quant:9:0 "
+            "unpack:14:1 unpack:15:1 o_quant:1:0 a_quant:12:0 unpack:14:0 unpack:15:0 a_quant:14:0 "
+            "o_quant:4:0 a_quant:13:0 o_quant:5:0 o_quant:0:0 a_quant:15:0 leave_t:14:0 leave_t:13:0 "
+            "o_quant:6:0 o_quant:2:0 leave:13:0 o_quant:7:0 ",
+            "g_keep:0:0 c_square:0:0 c_square:1:0 y_group:0:0 q_acc:1:0 c_square:2:0 c_square:3:0 "
+            "q_acc:0:0 y_group:1:0 q_acc:3:0 q_acc:5:0 q_acc:6:0 c_keep:1:0 q_acc:2:0 q_acc:4:0 "
+            "q_acc:7:0 q_acc:8:0 root:2:0 q_acc:9:0 q_acc:11:0 root:4:0 root:0:0 root:1:0 root:3:0 "
+            "q_acc:13:0 q_acc:10:0 root:6:0 root:7:0 row_c:0:0 root:5:0 expo:1:0 expo:5:0 expo:0:0 "
+            "expo:6:0 expo:3:0 expo:2:0 q_acc:14:0 expo:7:0 expo:4:0 q_acc:12:0 q_acc:15:0 root:10:0 "
+            "root:11:0 root:13:0 root:8:0 root:9:0 root:12:0 root:15:0 row_c:1:0 root:14:0 expo:8:0 "
+            "expo:9:0 expo:10:0 leave_t:5:0 leave:3:0 expo:11:0 expo:13:0 leave:5:0 leave_t:4:0 "
+            "expo:12:0 leave:7:0 leave:4:0 expo:14:0 expo:15:0 leave_t:7:0 leave:6:0 leave_t:6:0 "
+            "leave_t:8:0 leave_t:10:0 leave:8:0 leave:10:0 leave_t:9:0 leave:11:0 leave_t:11:0 "
+            "leave:9:0 leave_t:12:0 leave:12:0 leave:14:0 leave_t:15:0 leave:15:0 ",
+            "q_w:1:0 q_w:0:0 q_w:3:0 q_w:6:0 q_w:5:0 q_w:2:0 q_w:4:0 q_w:7:0 q_w:8:0 row_a:0:0 "
+            "row_a:2:0 q_w:9:0 row_a:4:0 q_w:11:0 row_a:3:0 row_a:1:0 q_w:13:0 row_a:6:0 q_w:10:0 "
+            "row_a:7:0 row_a:5:0 q_w:12:0 q_w:15:0 row_a:10:0 q_w:14:0 row_a:9:0 weigh:5:0 weigh:0:0 "
+            "weigh:1:0 row_a:8:0 row_a:11:0 row_a:13:0 row_a:12:0 weigh:2:0 weigh:7:0 weigh:3:0 "
+            "row_a:15:0 weigh:4:0 row_a:14:0 weigh:6:0 weigh:8:0 weigh:9:0 weigh:10:0 weigh:11:0 "
+            "weigh:13:0 weigh:12:0 weigh:15:0 ",
+        ]
+        queues = []
+        for text in orders:
+            queue = []
+            for word in text.split():
+                name, i, n = word.split(":")
+                queue.append((name, int(i), int(n)))
+            queues.append(queue)
+        room = {"x": 4, "o": 4, "og": 8, "art": 6}
+        made, done, at = {}, set(), [0, 0, 0, 0]
+        left = sum([len(z) for z in queues])
+        while left:
+            before = left
+            for k in range(4):
+                while at[k] < len(queues[k]):
+                    f, i, n = queues[k][at[k]]
+                    if not all([d in done for d in reads(f, i, n)]):
+                        break
+                    fresh = fills(f, i, n)
+                    free = True
+                    for e in range(len(fresh)):
+                        tag = fresh[e][0]
+                        m = len(made.setdefault(tag, [])) + e - room.get(tag, 3)
+                        if m >= 0 and not all([d in done for d in made[tag][m]]):
+                            free = False
+                    if not free:
+                        break
+                    for tag, readers in fresh:
+                        made[tag].append(readers)
+                    if f in ("cross", "dist", "turn", "unpack"):
+                        fns[f](i, n)
+                    else:
+                        fns[f](i)
+                    done.add((f, i, n))
+                    at[k] += 1
+                    left -= 1
+                if k == 0:
+                    continue
+            assert left < before, [queues[k][at[k]] if at[k] < len(queues[k]) else 0 for k in range(4)]

@@ -14,205 +14,279 @@ ACT = mybir.ActivationFunctionType
 
 B, N, E, C = 2048, 1024, 512, 512
 P = 128
-NT = B // P
-NP = NT // 2
+TILES = B // P
+PAIRS = TILES // 2
 FLOPS = 2 * B * N * E + 2 * B * N * C
 
-UNPACK_FIRST = [1,1,0,1,1,1,1,1,1,0,0,1,1,1,1,1]
-OG_FIRST = [1,2,5,7,8,10,12,14]
+KEEP_BELOW = 0.7
 FAR = 2.5e17
 TINY = 1e-12
 SPOT = 1.5
-H = 8
-LEAVE_V = [0,1,2,13]
-LEAVE_T_V = [0,1,2,3,13,14]
-SCALE_V = [14]
-KEEP_S = [1]
+HALF = 8
+
+ROOM = {
+    "bank_a": 4,
+    "bank_b": 4,
+    "grouped": 3,
+    "square": 5,
+    "ar": 3,
+    "ar_turned": 4,
+    "ar_codes": 4,
+    "result_grouped": 5,
+    "result": 6,
+    "result_codes": 8,
+}
+
+ORDER_TENSOR = (
+    "c_turn c_turn spread c_turn c_turn q_turn c_sum cross0 cross0 q_turn q_turn c_sum c_sum c_sum "
+    "cross0 q_turn cross0 cross1 cross1 q_sum q_turn cross1 cross0 q_sum cross1 cross0 cross1 q_turn "
+    "cross1 q_sum cross0 cross0 q_turn q_sum cross1 cross1 q_turn cross1 q_sum spread cross0 cross1 "
+    "q_sum cross0 cross0 cross1 q_sum cross0 cross0 cross1 cross0 cross1 cross0 q_sum turn cross1 "
+    "turn cross0 cross1 turn cross1 second_t second turn second_t second turn second_t turn second_t "
+    "turn second second_t second second turn second_t turn turn turn second second second_t second_t "
+    "second turn second_t second_t second second_t turn second second second turn turn second "
+    "second_t turn second second_t second_t second_t second_t second second"
+)
+ORDER_VECTOR = (
+    "c_scale c_scale c_quant q_scale q_quant c_quant c_scale q_scale q_quant c_keep c_scale c_quant "
+    "q_scale c_quant q_quant dist0 dist0 y_quant dist0 q_scale dist0 q_quant dist1 y_quant dist1 "
+    "q_keep low dist1 low q_scale q_keep row_inverse dist0 low dist1 dist0 row_inverse dist1 q_scale "
+    "q_keep row_inverse q_quant dist0 low dist1 low row_inverse low row_inverse dist0 dist1 dist1 "
+    "row_inverse q_keep q_scale low low row_inverse q_keep dist1 dist1 row_inverse q_quant dist0 "
+    "dist0 dist0 q_scale low low row_total q_keep dist0 row_inverse dist1 q_quant q_quant weigh "
+    "row_total row_inverse dist0 dist1 weigh row_total dist0 q_keep low dist0 dist1 weigh row_inverse "
+    "low row_total dist1 dist0 low row_inverse weigh q_keep row_total row_total row_inverse ar_quant "
+    "low dist1 ar_quant row_inverse dist1 low low row_total row_inverse weigh row_inverse ar_quant "
+    "row_total weigh result_quant weigh ar_quant leave ar_quant weigh leave_t row_total leave_t unpack "
+    "row_total weigh row_total ar_quant weigh leave weigh unpack ar_quant ar_quant row_total leave_t "
+    "ar_quant weigh unpack leave row_total ar_quant row_total ar_quant leave weigh row_total leave_t "
+    "ar_quant weigh weigh row_total ar_quant weigh ar_quant leave leave_t ar_quant result_quant result_quant "
+    "ar_quant result_quant result_quant result_quant result_quant leave result_quant"
+)
+ORDER_SCALAR = (
+    "c_squares c_squares c_squares q_square c_squares gain y_group q_square q_square y_group c_keep "
+    "q_square q_square root q_square q_square root root q_square root root root gain root row_slope "
+    "root expo expo expo expo expo expo expo expo unpack root root root unpack root unpack root "
+    "leave_t leave root leave_t unpack root row_slope root unpack expo expo expo leave leave leave_t "
+    "expo unpack expo unpack expo leave unpack leave_t leave_t expo unpack leave_t leave expo unpack "
+    "leave_t leave unpack leave unpack leave unpack leave leave_t leave_t leave_t leave_t leave"
+)
+ORDER_GPSIMD = "row_unit " * TILES
+
+ON_VECTOR = {
+    "c_keep": [0],
+    "unpack": [5, 7, 9],
+    "leave": [1, 2, 6, 7, 11, 14],
+    "leave_t": [2, 3, 5, 9, 11],
+}
 
 
 def tile_modernncastochasticneighbourregressor_x1_kernel(tc, q, c, g, h, y, u, r, out_0, out_1, out_2):
     nc = tc.nc
     with ExitStack() as ctx:
         keep = ctx.enter_context(tc.tile_pool(name="keep", bufs=1))
-        xs = ctx.enter_context(tc.tile_pool(name="xs", bufs=NT))
+        wide = ctx.enter_context(tc.tile_pool(name="wide", bufs=TILES))
         work = ctx.enter_context(tc.tile_pool(name="work", bufs=3))
-        mm = ctx.enter_context(tc.psum_pool(name="mm", bufs=2))
+        psum = ctx.enter_context(tc.psum_pool(name="psum", bufs=4))
 
-        ident = keep.tile([P, P], F32, name="ident")
-        g4 = keep.tile([P, 4], BF16, name="g4")
-        h4 = keep.tile([P, 4], BF16, name="h4")
-        gh = keep.tile([P, 4], F32, name="gh")
-        r8 = keep.tile([P, 2, 4], BF16, name="r8")
-        craw = keep.tile([P, 2, 4, E], BF16, name="craw")
-        yraw = keep.tile([P, 2, 4, C], BF16, name="yraw")
-        qraw = keep.tile([P, NT, E], BF16, name="qraw")
-        c2m = keep.tile([P, N], F32, name="c2m")
-        ch_codes = keep.tile([P, N], U32, name="ch_codes", align_bytes=64)
-        ch_scales = keep.tile([P, N], U8, name="ch_scales", align_bytes=64)
-        q_codes = keep.tile([P, B], U32, name="q_codes", align_bytes=64)
-        q_scales = keep.tile([P, B], U8, name="q_scales", align_bytes=64)
-        yg = keep.tile([P, 2, 4 * C], BF16, name="yg", align_bytes=64)
-        y_codes = keep.tile([P, 2, C], U32, name="y_codes", align_bytes=64)
-        y_scales = keep.tile([P, 2, C], U8, name="y_scales", align_bytes=64)
-        o_scales = keep.tile([P, B], U8, name="o_scales", align_bytes=64)
-        q2 = keep.tile([P, NT], F32, name="q2")
-        rows = keep.tile([P, 2 * E], BF16, name="rows")
+        identity = keep.tile([P, P], F32, name="identity")
+        make_identity(nc, identity[:])
         ones = keep.tile([P, P], BF16, name="ones")
         ones32 = keep.tile([P, P], F32, name="ones32")
-        urow = keep.tile([1, N], BF16, name="urow")
-        farrow = keep.tile([P, N], F32, name="farrow")
-        g_b = keep.tile([P, E], F32, name="g_b")
-        gh_b = keep.tile([P, E], F32, name="gh_b")
-        xmin = keep.tile([P, NT], F32, name="xmin")
-        xm = keep.tile([P, NT], F32, name="xm")
-        rk = keep.tile([P, NT], F32, name="rk")
-        w2 = keep.tile([P, NT], F32, name="w2")
-        nw = keep.tile([P, NT], F32, name="nw")
-        shift = keep.tile([P, NT], F32, name="shift")
-        ssum = keep.tile([P, NT], F32, name="ssum")
-        rs = keep.tile([P, NT], F32, name="rs")
-        x = [xs.tile([P, N], F32, name="x") for i in range(NT)]
+        r_row = keep.tile([P, N], BF16, name="r_row")
+        u_row = keep.tile([1, N], BF16, name="u_row")
+        far_row = keep.tile([P, N], F32, name="far_row")
+        g4 = keep.tile([P, 4], BF16, name="g4")
+        h8 = keep.tile([P, 8], BF16, name="h8")
+        gh = keep.tile([P, 4], F32, name="gh")
+        c_in = keep.tile([P, 2, 4, E], BF16, name="c_in")
+        y_in = keep.tile([P, 2, 4, C], BF16, name="y_in")
+        q_in = keep.tile([P, TILES, E], BF16, name="q_in")
+        r_all = keep.tile([P, N], F32, name="r_all")
+        c2 = keep.tile([P, N], F32, name="c2")
+        c_square = [keep.tile([P, 4, 512], F32, name="c_square%d" % a) for a in range(2)]
+        ch_codes = keep.tile([P, N], U32, name="ch_codes", align_bytes=64)
+        ch_scales = keep.tile([P, N], U8, name="ch_scales", align_bytes=64)
+        qg_codes = keep.tile([P, B], U32, name="qg_codes", align_bytes=64)
+        qg_scales = keep.tile([P, B], U8, name="qg_scales", align_bytes=64)
+        y_grouped = keep.tile([P, 2, 4 * C], BF16, name="y_grouped", align_bytes=64)
+        y_codes = keep.tile([P, 2, C], U32, name="y_codes", align_bytes=64)
+        y_scales = keep.tile([P, 2, C], U8, name="y_scales", align_bytes=64)
+        result_scales = keep.tile([P, B], U8, name="result_scales", align_bytes=64)
+        q2 = keep.tile([P, TILES], F32, name="q2")
+        least = keep.tile([P, TILES], F32, name="least")
+        unit = keep.tile([P, TILES], F32, name="unit")
+        per_unit = keep.tile([P, TILES], F32, name="per_unit")
+        slope = keep.tile([P, TILES], F32, name="slope")
+        minus_slope = keep.tile([P, TILES], F32, name="minus_slope")
+        shift = keep.tile([P, TILES], F32, name="shift")
+        total = keep.tile([P, TILES], F32, name="total")
+        per_total = keep.tile([P, TILES], F32, name="per_total")
+        x = [wide.tile([P, N], F32, name="x") for i in range(TILES)]
 
         ctx.enter_context(tc.manual_schedule())
 
-        make_identity(nc, ident[:])
-        nc.vector.memset(rows[:].bitcast(I32), 0)
-        nc.vector.memset(ones[:], 1.0)
-        nc.vector.memset(ones32[:], 1.0)
-        nc.gpsimd.memset(farrow[:], 0.0)
-        nc.scalar.dma_start(out=rows[0:1, 0:E], in_=g.unsqueeze(0))
-        nc.scalar.dma_start(out=rows[0:1, E : 2 * E], in_=h.unsqueeze(0))
-        nc.scalar.dma_start(out=h4[:], in_=h.rearrange("(p t) -> p t", t=4))
+        nc.scalar.dma_start(out=h8[:, 0:4], in_=h.rearrange("(p t) -> p t", t=4))
         nc.scalar.dma_start(out=g4[:], in_=g.rearrange("(p t) -> p t", t=4))
-        nc.scalar.dma_start(out=urow[:], in_=u.unsqueeze(0))
-        nc.scalar.dma_start(out=r8[:], in_=r.rearrange("(a p t) -> p a t", a=2, t=4))
+        nc.scalar.dma_start(out=u_row[:], in_=u.unsqueeze(0))
+        nc.gpsimd.memset(far_row[:], 0.0)
+        nc.vector.memset(ones32[:], 1.0)
+        nc.vector.memset(r_row[:].bitcast(I32), 0)
+        nc.vector.memset(ones[:], 1.0)
+        nc.scalar.dma_start(out=r_row[0:1, :], in_=r.unsqueeze(0))
         c_view = c.rearrange("(a p t) d -> a p t d", a=2, t=4)
         q_view = q.rearrange("(k p) d -> p k d", p=P)
         y_view = y.rearrange("(a p t) d -> a p t d", a=2, t=4)
         for a in range(2):
             for v in range(2):
-                nc.sync.dma_start(out=craw[:, a, 2 * v : 2 * v + 2, :], in_=c_view[a, :, 2 * v : 2 * v + 2, :])
-        for j in range(NP):
-            nc.sync.dma_start(out=qraw[:, 2 * j : 2 * j + 2, :], in_=q_view[:, 2 * j : 2 * j + 2, :])
-            if j == 3:
+                nc.sync.dma_start(out=c_in[:, a, 2 * v : 2 * v + 2, :], in_=c_view[a, :, 2 * v : 2 * v + 2, :])
+        for j in range(PAIRS):
+            nc.sync.dma_start(out=q_in[:, 2 * j : 2 * j + 2, :], in_=q_view[:, 2 * j : 2 * j + 2, :])
+            if j == PAIRS // 2 - 1:
                 for a in range(2):
-                    nc.sync.dma_start(out=yraw[:, a, :, :], in_=y_view[a])
-        nc.vector.tensor_tensor(out=gh[:], in0=g4[:], in1=h4[:], op=ALU.mult)
-        nc.vector.tensor_scalar(
-            out=farrow[0:1, :].rearrange("p (a t c) -> p a t c", a=2, t=4),
-            in0=urow[:].rearrange("p (a c t) -> p a t c", a=2, t=4),
-            scalar1=0.7,
-            scalar2=FAR,
-            op0=ALU.is_ge,
-            op1=ALU.mult,
-        )
+                    nc.sync.dma_start(out=y_in[:, a, :, :], in_=y_view[a])
+        nc.vector.tensor_copy(out=h8[:, 4:8], in_=h8[:, 0:4])
+        nc.vector.tensor_tensor(out=gh[:], in0=g4[:], in1=h8[:, 0:4], op=ALU.mult)
+        for a in range(2):
+            for v in range(2):
+                s = 512 * a + 256 * v
+                nc.vector.tensor_scalar(
+                    out=far_row[0:1, s : s + 256].rearrange("p (e c) -> p e c", e=2),
+                    in0=u_row[:, 512 * a : 512 * a + 512].rearrange("p (c v e) -> p v e c", v=2, e=2)[:, v, :, :],
+                    scalar1=KEEP_BELOW,
+                    scalar2=FAR,
+                    op0=ALU.is_ge,
+                    op1=ALU.mult,
+                )
 
-        tiles = {}
-
-        depth = {"x": 4, "o": 4}
+        made = {}
 
         def bank(tag, *key):
-            t = mm.tile([P, 512], F32, name=tag, bufs=depth[tag])
-            tiles[key] = t
-            return t
+            made[key] = psum.tile([P, 512], F32, name=tag, bufs=ROOM[tag])
+            return made[key]
 
-        def head_bank(*key):
-            return bank("o", *key)
+        def rotating(tag, shape, dtype, *key):
+            made[key] = work.tile(shape, dtype, name=tag, bufs=ROOM[tag], align_bytes=64)
+            return made[key]
 
-        def turn_rows(key, rows):
-            t = head_bank(*key)
-            for w in range(2):
-                for k in range(2):
-                    s = w * 256 + k * P
-                    nc.tensor.transpose(t[:, s : s + P], rows[k].bitcast(F32)[:, w : E // 2 : 2], ident[:])
 
-        def scale_rows(key, factor):
-            t = work.tile([P, 1024], BF16, name="grp", align_bytes=64)
-            tiles["grp", key] = t
+        def spread(a):
+            t = bank("bank_a", "spread", a)
+            nc.tensor.matmul(t[:], lhsT=ones[:], rhs=r_row[:, 512 * a : 512 * a + 512], start=True, stop=True)
+
+        def gain(a):
+            nc.scalar.copy(
+                out=r_all[:, 512 * a : 512 * a + 512].rearrange("p (v c e) -> p v c e", v=2, e=2),
+                in_=made["spread", a][:].rearrange("p (c v e) -> p v c e", v=2, e=2),
+            )
+
+
+        def c_turn(k):
+            t = bank("bank_b", "c", k)
+            for e in range(2):
+                words = c_in[:, k // 2, 2 * (k % 2) + e, :].bitcast(F32)
+                for w in range(2):
+                    s = (2 * e + w) * P
+                    nc.tensor.transpose(t[:, s : s + P], words[:, w : E // 2 : 2], identity[:])
+
+        def c_scale(k):
+            t = rotating("grouped", [P, 1024], BF16, "ch", k)
             nc.vector.tensor_tensor(
-                out=t[:].rearrange("p (r w d) -> p r w d", w=2, d=2),
-                in0=tiles[key][:].bitcast(BF16).rearrange("p (w r d) -> p r w d", w=2, d=2),
-                in1=factor[:].rearrange("p (w d) -> p w d", d=2).unsqueeze(1).to_broadcast([P, 256, 2, 2]),
+                out=t[:].rearrange("p (c x d) -> p c x d", x=4, d=2),
+                in0=made["c", k][:].bitcast(BF16).rearrange("p (x c d) -> p c x d", x=4, d=2),
+                in1=h8[:].rearrange("p (x d) -> p x d", d=2).unsqueeze(1).to_broadcast([P, P, 4, 2]),
                 op=ALU.mult,
             )
 
-        def quantise(codes, scales, key, j):
-            s = slice(256 * j, 256 * j + 256)
-            nc.vector.quantize_mx(out=codes[:, s].bitcast(FP8X4), scales=scales[:, s], in_=tiles["grp", key][:])
-
-        def c_turn(k):
-            turn_rows(("c", k), [craw[:, k // 2, 2 * (k % 2) + e, :] for e in range(2)])
-
-        def c_scale(k):
-            scale_rows(("c", k), h4)
-
-        def gb(i):
-            for k in range(2):
-                t = head_bank("gb", k)
-                nc.tensor.matmul(t[:], lhsT=ones[:], rhs=rows[:, E * k : E * k + E], start=True, stop=True)
-
-        def g_keep(i):
-            nc.scalar.copy(out=g_b[:], in_=tiles["gb", 0][:])
-
-        def gh_mul(i):
-            nc.vector.tensor_tensor(out=gh_b[:], in0=tiles["gb", 1][:], in1=g_b[:], op=ALU.mult)
-
-        def c_square(k):
-            b16 = tiles["c", k][:].bitcast(BF16).rearrange("p (w r d) -> p w r d", w=2, d=2)
-            t = work.tile([P, 4, 256], F32, name="sq", bufs=4)
-            tiles["sq", k] = t
+        def c_squares(k):
+            bits = made["c", k][:].bitcast(BF16).rearrange("p (e w c d) -> p w e c d", e=2, w=2, d=2)
+            s = slice(256 * (k % 2), 256 * (k % 2) + 256)
             for d in range(2):
-                nc.scalar.activation(out=t[:, d:4:2, :], in_=b16[:, :, :, d], func=ACT.Square)
+                nc.scalar.activation(
+                    out=c_square[k // 2][:, d:4:2, s].rearrange("p w (e c) -> p w e c", e=2),
+                    in_=bits[:, :, :, :, d],
+                    func=ACT.Square,
+                )
 
         def c_quant(k):
-            quantise(ch_codes, ch_scales, ("c", k), k)
+            s = slice(256 * k, 256 * k + 256)
+            nc.vector.quantize_mx(out=ch_codes[:, s].bitcast(FP8X4), scales=ch_scales[:, s], in_=made["ch", k][:])
 
         def c_sum(k):
-            if ("c2", k // 2) not in tiles:
-                bank("x", "c2", k // 2)
+            a = k // 2
+            if ("c2", a) not in made:
+                bank("bank_a", "c2", a)
             s = slice(256 * (k % 2), 256 * (k % 2) + 256)
-            t = tiles["c2", k // 2]
-            nc.tensor.matmul(t[:, s], lhsT=ones32[:], rhs=farrow[:, 256 * k : 256 * k + 256], start=True, stop=False)
+            t = made["c2", a]
+            nc.tensor.matmul(t[:, s], lhsT=ones32[:], rhs=far_row[:, 256 * k : 256 * k + 256], start=True, stop=False)
             for m in range(4):
                 nc.tensor.matmul(
                     t[:, s],
                     lhsT=gh[:, m : m + 1].to_broadcast([P, P]),
-                    rhs=tiles["sq", k][:, m, :],
+                    rhs=c_square[a][:, m, s],
                     start=False,
                     stop=(m == 3),
                 )
 
         def c_keep(a):
-            copy = nc.scalar.copy if a in KEEP_S else nc.vector.tensor_copy
-            copy(out=c2m[:, 512 * a : 512 * a + 512], in_=tiles["c2", a][:])
+            copy = nc.vector.tensor_copy if a in ON_VECTOR["c_keep"] else nc.scalar.copy
+            copy(
+                out=c2[:, 512 * a : 512 * a + 512].rearrange("p (v c e) -> p v c e", v=2, e=2),
+                in_=made["c2", a][:].rearrange("p (v e c) -> p v c e", v=2, e=2),
+            )
+
 
         def q_turn(j):
-            turn_rows(("q", j), [qraw[:, 2 * j + k, :] for k in range(2)])
+            t = bank("bank_b", "q", j)
+            for w in range(2):
+                for k in range(2):
+                    s = w * 256 + k * P
+                    words = q_in[:, 2 * j + k, :].bitcast(F32)
+                    nc.tensor.transpose(t[:, s : s + P], words[:, w : E // 2 : 2], identity[:])
 
         def q_scale(j):
-            scale_rows(("q", j), g4)
+            t = rotating("grouped", [P, 1024], BF16, "qg", j)
+            nc.vector.tensor_tensor(
+                out=t[:].rearrange("p (b w d) -> p b w d", w=2, d=2),
+                in0=made["q", j][:].bitcast(BF16).rearrange("p (w b d) -> p b w d", w=2, d=2),
+                in1=g4[:].rearrange("p (w d) -> p w d", d=2).unsqueeze(1).to_broadcast([P, 256, 2, 2]),
+                op=ALU.mult,
+            )
+
+        def q_square(j):
+            bits = made["q", j][:].bitcast(BF16).rearrange("p (w b d) -> p w b d", w=2, d=2)
+            t = rotating("square", [P, 4, 256], F32, "q_square", j)
+            for d in range(2):
+                nc.scalar.activation(out=t[:, d:4:2, :], in_=bits[:, :, :, d], func=ACT.Square)
 
         def q_quant(j):
-            quantise(q_codes, q_scales, ("q", j), j)
+            s = slice(256 * j, 256 * j + 256)
+            nc.vector.quantize_mx(out=qg_codes[:, s].bitcast(FP8X4), scales=qg_scales[:, s], in_=made["qg", j][:])
 
-        def q_w(i):
-            t = work.tile([P, E], F32, name="qw")
-            tiles["qw", i] = t
-            nc.gpsimd.tensor_tensor(out=t[:], in0=qraw[:, i, :], in1=gh_b[:], op=ALU.mult)
-            nc.gpsimd.tensor_tensor(out=t[:], in0=t[:], in1=qraw[:, i, :], op=ALU.mult)
+        def q_sum(j):
+            t = bank("bank_b", "q2", j)
+            for k in range(2):
+                for m in range(4):
+                    nc.tensor.matmul(
+                        t[:, k : k + 1],
+                        lhsT=made["q_square", j][:, m, k * P : k * P + P],
+                        rhs=gh[:, m : m + 1],
+                        start=(m == 0),
+                        stop=(m == 3),
+                    )
 
-        def q_acc(i):
-            t = tiles["qw", i]
-            nc.scalar.activation(out=t[:], in_=t[:], func=ACT.Copy, accum_out=q2[:, i : i + 1])
+        def q_keep(j):
+            nc.vector.tensor_copy(out=q2[:, 2 * j : 2 * j + 2], in_=made["q2", j][:, 0:2])
+
 
         def cross(i, n):
-            t = bank("x", "cross", i, n)
+            t = bank("bank_a", "cross", i, n)
             b = slice(P * i, P * i + P)
             s = slice(512 * n, 512 * n + 512)
             nc.tensor.matmul_mx(
                 out=t[:],
-                lhsT=q_codes[:, b].bitcast(FP8X4),
-                lhsT_scale=q_scales[:, b],
+                lhsT=qg_codes[:, b].bitcast(FP8X4),
+                lhsT_scale=qg_scales[:, b],
                 rhs=ch_codes[:, s].bitcast(FP8X4),
                 rhs_scale=ch_scales[:, s],
                 start=True,
@@ -222,7 +296,7 @@ def tile_modernncastochasticneighbourregressor_x1_kernel(tc, q, c, g, h, y, u, r
         def dist(i, n):
             s = slice(512 * n, 512 * n + 512)
             nc.vector.scalar_tensor_tensor(
-                out=x[i][:, s], in0=tiles["cross", i, n][:], scalar=-2.0, in1=c2m[:, s], op0=ALU.mult, op1=ALU.add
+                out=x[i][:, s], in0=made["cross", i, n][:], scalar=-2.0, in1=c2[:, s], op0=ALU.mult, op1=ALU.add
             )
 
         def low(i):
@@ -233,107 +307,109 @@ def tile_modernncastochasticneighbourregressor_x1_kernel(tc, q, c, g, h, y, u, r
                 scalar2=None,
                 op0=ALU.add,
                 op1=ALU.min,
-                accum_out=xmin[:, i : i + 1],
+                accum_out=least[:, i : i + 1],
             )
 
-        def row_a(i):
+        def row_unit(i):
             s = slice(i, i + 1)
             nc.gpsimd.tensor_scalar(
-                out=xm[:, s], in0=xmin[:, s], scalar1=TINY, scalar2=1.0 / SPOT, op0=ALU.max, op1=ALU.mult
+                out=unit[:, s], in0=least[:, s], scalar1=TINY, scalar2=1.0 / SPOT, op0=ALU.max, op1=ALU.mult
             )
 
-        def row_b(i):
-            s = slice(i, i + 1)
-            nc.vector.reciprocal(out=rk[:, s], in_=xm[:, s])
-
-        def row_c(i):
-            s = slice(0, H) if i == 0 else slice(H, NT)
-            nc.scalar.activation(out=w2[:, s], in_=xm[:, s], func=ACT.Sqrt, scale=4.0)
-            nc.gpsimd.tensor_scalar(out=nw[:, s], in0=w2[:, s], scalar1=-1.0, scalar2=0.0, op0=ALU.mult, op1=ALU.add)
-            nc.gpsimd.tensor_scalar(
-                out=shift[:, s], in0=w2[:, s], scalar1=SPOT**0.5, scalar2=0.0, op0=ALU.mult, op1=ALU.add
-            )
+        def row_inverse(i):
+            nc.vector.reciprocal(out=per_unit[:, i : i + 1], in_=unit[:, i : i + 1])
 
         def root(i):
-            nc.scalar.activation(out=x[i][:], in_=x[i][:], func=ACT.Sqrt, scale=rk[:, i : i + 1])
+            nc.scalar.activation(out=x[i][:], in_=x[i][:], func=ACT.Sqrt, scale=per_unit[:, i : i + 1])
 
-        def y_group(a):
-            out = yg[:, a, :].rearrange("p (t c j) -> p t c j", t=4, j=4)
-            in_ = yraw[:, a, :, :].rearrange("p j (c t) -> p t c j", t=4)
-            nc.scalar.copy(out=out, in_=in_)
-
-        def y_quant(a):
-            nc.vector.quantize_mx(out=y_codes[:, a, :].bitcast(FP8X4), scales=y_scales[:, a, :], in_=yg[:, a, :])
+        def row_slope(k):
+            s = slice(0, HALF) if k == 0 else slice(HALF, TILES)
+            nc.scalar.activation(out=slope[:, s], in_=unit[:, s], func=ACT.Sqrt, scale=4.0)
+            nc.gpsimd.tensor_scalar(
+                out=minus_slope[:, s], in0=slope[:, s], scalar1=-1.0, scalar2=0.0, op0=ALU.mult, op1=ALU.add
+            )
+            nc.gpsimd.tensor_scalar(
+                out=shift[:, s], in0=slope[:, s], scalar1=SPOT**0.5, scalar2=0.0, op0=ALU.mult, op1=ALU.add
+            )
 
         def expo(i):
             nc.scalar.activation(
                 out=x[i][:],
                 in_=x[i][:],
                 func=ACT.Exp,
-                scale=nw[:, i : i + 1],
+                scale=minus_slope[:, i : i + 1],
                 bias=shift[:, i : i + 1],
-                accum_out=ssum[:, i : i + 1],
+                accum_out=total[:, i : i + 1],
             )
 
-        def inv(i):
-            nc.vector.reciprocal(out=rs[:, i : i + 1], in_=ssum[:, i : i + 1])
+        def row_total(i):
+            nc.vector.reciprocal(out=per_total[:, i : i + 1], in_=total[:, i : i + 1])
+
+
+        def y_group(a):
+            nc.scalar.copy(
+                out=y_grouped[:, a, :].rearrange("p (m c t) -> p m c t", m=4, t=4),
+                in_=y_in[:, a, :, :].rearrange("p t (c m) -> p m c t", m=4),
+            )
+
+        def y_quant(a):
+            nc.vector.quantize_mx(
+                out=y_codes[:, a, :].bitcast(FP8X4), scales=y_scales[:, a, :], in_=y_grouped[:, a, :]
+            )
+
 
         def weigh(i):
-            if i in SCALE_V:
-                nc.vector.tensor_scalar(out=x[i][:], in0=x[i][:], scalar1=rs[:, i : i + 1], scalar2=None, op0=ALU.mult)
-            else:
-                for n in range(1):
-                    s = slice(1024 * n, 1024 * (n + 1))
-                    nc.gpsimd.tensor_scalar(
-                        out=x[i][:, s], in0=x[i][:, s], scalar1=rs[:, i : i + 1], scalar2=1.0, op0=ALU.mult, op1=ALU.mult
-                    )
-
-        def turn(i, n):
-            t = bank("x", "a", i, n)
-            for k in range(4):
-                s = 512 * n + P * k
-                nc.tensor.transpose(t[:, P * k : P * k + P], x[i][:, s : s + P], ident[:])
-
-        def unpack(i, n):
-            if n == UNPACK_FIRST[i]:
-                t = work.tile([P, 1024], BF16, name="art", bufs=6, align_bytes=64)
-                tiles["art", i] = t
-            nc.vector.tensor_tensor(
-                out=tiles["art", i][:, 512 * n : 512 * n + 512].rearrange("p (b t) -> p b t", t=4),
-                in0=tiles["a", i, n][:].rearrange("p (t b) -> p b t", t=4),
-                in1=r8[:, n, :].unsqueeze(1).to_broadcast([P, P, 4]),
-                op=ALU.mult,
+            t = rotating("ar", [P, N], BF16, "ar", i)
+            nc.vector.scalar_tensor_tensor(
+                out=t[:], in0=x[i][:], scalar=per_total[:, i : i + 1], in1=r_all[:], op0=ALU.mult, op1=ALU.mult
             )
 
-        def a_quant(i):
-            k = work.tile([P, 256], U32, name="art_codes", align_bytes=64)
-            s = work.tile([P, 256], U8, name="art_scales", align_bytes=64)
-            tiles["codes", i], tiles["scales", i] = k, s
-            nc.vector.quantize_mx(out=k[:].bitcast(FP8X4), scales=s[:], in_=tiles["art", i][:])
+        def turn(i):
+            t = bank("bank_a", "ar_bank", i)
+            words = made["ar", i][:].bitcast(F32)
+            for k in range(4):
+                nc.tensor.transpose(t[:, P * k : P * k + P], words[:, P * k : P * k + P], identity[:])
 
-        def second(i):
-            tt = bank("o", "ot", i)
-            k, s = tiles["codes", i], tiles["scales", i]
+        def unpack(i):
+            t = rotating("ar_turned", [P, 1024], BF16, "ar_turned", i)
+            copy = nc.vector.tensor_copy if i in ON_VECTOR["unpack"] else nc.scalar.copy
+            copy(
+                out=t[:].bitcast(F32).rearrange("p (a b v) -> p a b v", a=2, v=2),
+                in_=made["ar_bank", i][:].rearrange("p (a v b) -> p a b v", a=2, v=2),
+            )
+
+        def ar_quant(i):
+            codes = rotating("ar_codes", [P, 256], U32, "ar_codes", i)
+            scales = work.tile([P, 256], U8, name="ar_scales", bufs=ROOM["ar_codes"], align_bytes=64)
+            made["ar_scales", i] = scales
+            nc.vector.quantize_mx(out=codes[:].bitcast(FP8X4), scales=scales[:], in_=made["ar_turned", i][:])
+
+        def second_t(i):
+            t = bank("bank_b", "result_t_bank", i)
+            codes, scales = made["ar_codes", i], made["ar_scales", i]
             for m in range(4):
+                s = slice(P * m, P * m + P)
                 for a in range(2):
+                    k = slice(P * a, P * a + P)
                     nc.tensor.matmul_mx(
-                        out=tt[:, P * m : P * m + P],
-                        lhsT=y_codes[:, a, P * m : P * m + P].bitcast(FP8X4),
-                        lhsT_scale=y_scales[:, a, P * m : P * m + P],
-                        rhs=k[:, P * a : P * a + P].bitcast(FP8X4),
-                        rhs_scale=s[:, P * a : P * a + P],
+                        out=t[:, s],
+                        lhsT=y_codes[:, a, s].bitcast(FP8X4),
+                        lhsT_scale=y_scales[:, a, s],
+                        rhs=codes[:, k].bitcast(FP8X4),
+                        rhs_scale=scales[:, k],
                         start=(a == 0),
                         stop=(a == 1),
                     )
 
-        def third(i):
-            t = bank("o", "o", i)
-            k, s = tiles["codes", i], tiles["scales", i]
+        def second(i):
+            t = bank("bank_b", "result_bank", i)
+            codes, scales = made["ar_codes", i], made["ar_scales", i]
             for a in range(2):
+                k = slice(P * a, P * a + P)
                 nc.tensor.matmul_mx(
                     out=t[:],
-                    lhsT=k[:, P * a : P * a + P].bitcast(FP8X4),
-                    lhsT_scale=s[:, P * a : P * a + P],
+                    lhsT=codes[:, k].bitcast(FP8X4),
+                    lhsT_scale=scales[:, k],
                     rhs=y_codes[:, a, :].bitcast(FP8X4),
                     rhs_scale=y_scales[:, a, :],
                     start=(a == 0),
@@ -341,227 +417,143 @@ def tile_modernncastochasticneighbourregressor_x1_kernel(tc, q, c, g, h, y, u, r
                 )
 
         def leave(i):
-            t = work.tile([P, C], F32, name="o", bufs=6)
-            copy = nc.vector.tensor_copy if i in LEAVE_V else nc.scalar.copy
-            copy(out=t[:].rearrange("p (c m) -> p c m", m=4), in_=tiles["o", i][:].rearrange("p (m c) -> p c m", m=4))
+            t = rotating("result", [P, C], F32, "result", i)
+            copy = nc.vector.tensor_copy if i in ON_VECTOR["leave"] else nc.scalar.copy
+            copy(out=t[:].rearrange("p (c m) -> p c m", m=4), in_=made["result_bank", i][:].rearrange("p (m c) -> p c m", m=4))
             nc.sync.dma_start(out=out_0[P * i : P * i + P, :], in_=t[:])
 
         def leave_t(i):
-            if i == OG_FIRST[i // 2]:
-                og = work.tile([P, 1024], BF16, name="og", bufs=8, align_bytes=64)
-                tiles["og", i // 2] = og
-            copy = nc.vector.tensor_copy if i in LEAVE_T_V else nc.scalar.copy
+            if ("result_grouped", i // 2) not in made:
+                rotating("result_grouped", [P, 1024], BF16, "result_grouped", i // 2)
+            s = slice(512 * (i % 2), 512 * (i % 2) + 512)
+            copy = nc.vector.tensor_copy if i in ON_VECTOR["leave_t"] else nc.scalar.copy
             copy(
-                out=tiles["og", i // 2][:, 512 * (i % 2) : 512 * (i % 2) + 512].rearrange("p (b m) -> p b m", m=4),
-                in_=tiles["ot", i][:].rearrange("p (m b) -> p b m", m=4),
+                out=made["result_grouped", i // 2][:, s].rearrange("p (b m) -> p b m", m=4),
+                in_=made["result_t_bank", i][:].rearrange("p (m b) -> p b m", m=4),
             )
 
-        stored = []
-
-        def o_quant(j):
-            k = work.tile([P, 256], U32, name="o_codes", bufs=8, align_bytes=64)
+        def result_quant(j):
+            t = rotating("result_codes", [P, 256], U32, "result_codes", j)
             s = slice(256 * j, 256 * j + 256)
-            nc.vector.quantize_mx(out=k[:].bitcast(FP8X4), scales=o_scales[:, s], in_=tiles["og", j][:])
+            nc.vector.quantize_mx(out=t[:].bitcast(FP8X4), scales=result_scales[:, s], in_=made["result_grouped", j][:])
             nc.sync.dma_start(
-                out=out_1[0, :, s, :].rearrange("p m t -> p (m t)").bitcast(I32), in_=k[:].bitcast(I32)
+                out=out_1[0, :, s, :].rearrange("p m t -> p (m t)").bitcast(I32), in_=t[:].bitcast(I32)
             )
-            stored.append(j)
-            half = [k for k in stored if k // 4 == j // 4]
-            if len(half) == 4:
-                s = slice(1024 * (j // 4), 1024 * (j // 4) + 1024)
+            if j % 4 == 3:
+                s = slice(256 * (j - 3), 256 * j + 256)
                 for b in range(4):
                     nc.sync.dma_start(
-                        out=out_2[0, 4 * b : 4 * b + 4, s].bitcast(I32), in_=o_scales[32 * b : 32 * b + 4, s].bitcast(I32)
+                        out=out_2[0, 4 * b : 4 * b + 4, s].bitcast(I32), in_=result_scales[32 * b : 32 * b + 4, s].bitcast(I32)
                     )
 
-        fns = {
-            "gb": gb, "g_keep": g_keep, "gh_mul": gh_mul, "c_turn": c_turn, "c_scale": c_scale, "c_square": c_square, "c_quant": c_quant,
-            "c_sum": c_sum, "c_keep": c_keep, "q_turn": q_turn, "q_scale": q_scale, "q_quant": q_quant, "q_w": q_w, "q_acc": q_acc,
-            "cross": cross, "dist": dist, "low": low, "row_a": row_a, "row_b": row_b, "row_c": row_c, "root": root, "y_group": y_group,
-            "y_quant": y_quant, "expo": expo, "inv": inv, "weigh": weigh, "turn": turn, "unpack": unpack, "a_quant": a_quant,
-            "second": second, "third": third, "leave": leave, "leave_t": leave_t, "o_quant": o_quant,
+        def both(name, i):
+            return [(name, 2 * i), (name, 2 * i + 1)]
+
+        def nothing(i):
+            return []
+
+        steps = {
+            "spread": (spread, nothing, lambda i: [("bank_a", [("gain", i)])]),
+            "gain": (gain, lambda i: [("spread", i)], nothing),
+            "c_turn": (c_turn, nothing, lambda i: [("bank_b", [("c_scale", i), ("c_squares", i)])]),
+            "c_scale": (c_scale, lambda i: [("c_turn", i)], lambda i: [("grouped", [("c_quant", i)])]),
+            "c_squares": (c_squares, lambda i: [("c_turn", i)], nothing),
+            "c_quant": (c_quant, lambda i: [("c_scale", i)], nothing),
+            "c_sum": (c_sum, lambda i: [("c_squares", i)], lambda i: [("bank_a", [("c_keep", i // 2)])] if i % 2 == 0 else []),
+            "c_keep": (c_keep, lambda i: both("c_sum", i), nothing),
+            "q_turn": (q_turn, nothing, lambda i: [("bank_b", [("q_scale", i), ("q_square", i)])]),
+            "q_scale": (q_scale, lambda i: [("q_turn", i)], lambda i: [("grouped", [("q_quant", i)])]),
+            "q_square": (q_square, lambda i: [("q_turn", i)], lambda i: [("square", [("q_sum", i)])]),
+            "q_quant": (q_quant, lambda i: [("q_scale", i)], nothing),
+            "q_sum": (q_sum, lambda i: [("q_square", i)], lambda i: [("bank_b", [("q_keep", i)])]),
+            "q_keep": (q_keep, lambda i: [("q_sum", i)], nothing),
+            "cross0": (
+                lambda i: cross(i, 0),
+                lambda i: [("q_quant", i // 2)] + both("c_quant", 0),
+                lambda i: [("bank_a", [("dist0", i)])],
+            ),
+            "cross1": (
+                lambda i: cross(i, 1),
+                lambda i: [("q_quant", i // 2)] + both("c_quant", 1),
+                lambda i: [("bank_a", [("dist1", i)])],
+            ),
+            "dist0": (lambda i: dist(i, 0), lambda i: [("cross0", i), ("c_keep", 0)], nothing),
+            "dist1": (lambda i: dist(i, 1), lambda i: [("cross1", i), ("c_keep", 1)], nothing),
+            "low": (low, lambda i: [("dist0", i), ("dist1", i), ("q_keep", i // 2)], nothing),
+            "row_unit": (row_unit, lambda i: [("low", i)], nothing),
+            "row_inverse": (row_inverse, lambda i: [("row_unit", i)], nothing),
+            "root": (root, lambda i: [("row_inverse", i)], nothing),
+            "row_slope": (
+                row_slope,
+                lambda k: [("row_unit", i) for i in (range(HALF) if k == 0 else range(HALF, TILES))],
+                nothing,
+            ),
+            "expo": (expo, lambda i: [("root", i), ("row_slope", 0 if i < HALF else 1)], nothing),
+            "row_total": (row_total, lambda i: [("expo", i)], nothing),
+            "y_group": (y_group, nothing, nothing),
+            "y_quant": (y_quant, lambda i: [("y_group", i)], nothing),
+            "weigh": (
+                weigh,
+                lambda i: [("row_total", i)] + both("gain", 0),
+                lambda i: [("ar", [("turn", i)])],
+            ),
+            "turn": (turn, lambda i: [("weigh", i)], lambda i: [("bank_a", [("unpack", i)])]),
+            "unpack": (unpack, lambda i: [("turn", i)], lambda i: [("ar_turned", [("ar_quant", i)])]),
+            "ar_quant": (
+                ar_quant,
+                lambda i: [("unpack", i)],
+                lambda i: [("ar_codes", [("second_t", i), ("second", i)])],
+            ),
+            "second_t": (
+                second_t,
+                lambda i: [("ar_quant", i)] + both("y_quant", 0),
+                lambda i: [("bank_b", [("leave_t", i)])],
+            ),
+            "second": (
+                second,
+                lambda i: [("ar_quant", i)] + both("y_quant", 0),
+                lambda i: [("bank_b", [("leave", i)])],
+            ),
+            "leave": (leave, lambda i: [("second", i)], nothing),
+            "leave_t": (
+                leave_t,
+                lambda i: [("second_t", i)] + ([("leave_t", i - 1)] if i % 2 else []),
+                lambda i: [("result_grouped", [("result_quant", i // 2)])] if i % 2 == 0 else [],
+            ),
+            "result_quant": (result_quant, lambda i: both("leave_t", i), nothing),
         }
 
-        def reads(f, i, n):
-            if f in ("g_keep",):
-                return [("gb", 0, 0)]
-            if f == "gh_mul":
-                return [("g_keep", 0, 0)]
-            if f in ("c_scale", "c_square"):
-                return [("c_turn", i, 0)]
-            if f == "c_quant":
-                return [("c_scale", i, 0)]
-            if f == "c_sum":
-                return [("c_square", i, 0)]
-            if f == "c_keep":
-                return [("c_sum", 2 * i, 0), ("c_sum", 2 * i + 1, 0)]
-            if f == "q_scale":
-                return [("q_turn", i, 0)]
-            if f == "q_quant":
-                return [("q_scale", i, 0)]
-            if f == "q_w":
-                return [("gh_mul", 0, 0)]
-            if f == "q_acc":
-                return [("q_w", i, 0)]
-            if f == "cross":
-                return [("q_quant", i // 2, 0), ("c_quant", 2 * n, 0), ("c_quant", 2 * n + 1, 0)]
-            if f == "dist":
-                return [("cross", i, n), ("c_keep", n, 0)]
-            if f == "low":
-                return [("dist", i, 0), ("dist", i, 1), ("q_acc", i, 0)]
-            if f == "row_a":
-                return [("low", i, 0)]
-            if f == "row_b":
-                return [("row_a", i, 0)]
-            if f == "row_c":
-                return [("row_a", k, 0) for k in (range(H) if i == 0 else range(H, NT))]
-            if f == "root":
-                return [("row_b", i, 0)]
-            if f == "y_quant":
-                return [("y_group", i, 0)]
-            if f == "expo":
-                return [("root", i, 0), ("row_c", 0 if i < H else 1, 0)]
-            if f == "inv":
-                return [("expo", i, 0)]
-            if f == "weigh":
-                return [("inv", i, 0)]
-            if f == "turn":
-                return [("weigh", i, 0)]
-            if f == "unpack":
-                return [("turn", i, n)]
-            if f == "a_quant":
-                return [("unpack", i, 0), ("unpack", i, 1)]
-            if f in ("second", "third"):
-                return [("a_quant", i, 0), ("y_quant", 0, 0), ("y_quant", 1, 0)]
-            if f == "leave":
-                return [("third", i, 0)]
-            if f == "leave_t":
-                first = OG_FIRST[i // 2]
-                return [("second", i, 0)] + ([] if i == first else [("leave_t", first, 0)])
-            if f == "o_quant":
-                return [("leave_t", 2 * i, 0), ("leave_t", 2 * i + 1, 0)]
-            return []
-
-        def fills(f, i, n):
-            if f == "c_turn":
-                return [("o", [("c_scale", i, 0), ("c_square", i, 0)])]
-            if f == "gb":
-                return [("o", [("g_keep", 0, 0)]), ("o", [("gh_mul", 0, 0)])]
-            if f == "q_turn":
-                return [("o", [("q_scale", i, 0)])]
-            if f == "c_sum" and ("c_sum", i ^ 1, 0) not in done:
-                return [("x", [("c_keep", i // 2, 0)])]
-            if f == "cross":
-                return [("x", [("dist", i, n)])]
-            if f == "turn":
-                return [("x", [("unpack", i, n)])]
-            if f == "second":
-                return [("o", [("leave_t", i, 0)])]
-            if f == "third":
-                return [("o", [("leave", i, 0)])]
-            if f == "c_scale":
-                return [("grp", [("c_quant", i, 0)])]
-            if f == "q_scale":
-                return [("grp", [("q_quant", i, 0)])]
-            if f == "q_w":
-                return [("qw", [("q_acc", i, 0)])]
-            if f == "unpack" and n == UNPACK_FIRST[i]:
-                return [("art", [("a_quant", i, 0)])]
-            if f == "a_quant":
-                return [("codes", [("second", i, 0), ("third", i, 0)])]
-            if f == "leave_t" and i == OG_FIRST[i // 2]:
-                return [("og", [("o_quant", i // 2, 0)])]
-            return []
-
-        orders = [
-            "gb:0:0 c_turn:0:0 q_turn:0:0 q_turn:2:0 c_turn:1:0 c_sum:0:0 q_turn:1:0 c_turn:3:0 "
-            "c_turn:2:0 q_turn:3:0 c_sum:1:0 cross:0:0 cross:4:0 c_sum:3:0 c_sum:2:0 q_turn:4:0 "
-            "cross:2:1 cross:2:0 cross:0:1 cross:3:1 cross:6:1 q_turn:7:0 cross:4:1 cross:1:1 cross:3:0 "
-            "cross:6:0 cross:1:0 cross:5:0 cross:5:1 cross:7:0 q_turn:5:0 q_turn:6:0 cross:7:1 "
-            "cross:10:0 cross:8:0 cross:10:1 cross:9:1 cross:9:0 cross:11:1 cross:8:1 cross:12:0 "
-            "cross:12:1 cross:13:1 cross:11:0 cross:13:0 turn:0:1 cross:15:1 cross:14:1 turn:0:0 "
-            "turn:1:1 cross:15:0 turn:1:0 cross:14:0 turn:5:1 turn:2:0 turn:2:1 third:0:0 second:0:0 "
-            "turn:3:1 turn:3:0 second:1:0 turn:5:0 turn:4:0 third:1:0 turn:4:1 turn:7:0 turn:7:1 "
-            "second:2:0 second:3:0 second:5:0 third:3:0 third:2:0 turn:6:1 turn:6:0 third:5:0 "
-            "second:4:0 third:4:0 turn:9:0 turn:8:1 turn:8:0 turn:10:0 third:7:0 second:7:0 turn:10:1 "
-            "turn:9:1 third:6:0 turn:11:1 turn:13:1 turn:11:0 second:6:0 second:10:0 turn:13:0 "
-            "turn:12:0 turn:12:1 second:8:0 third:10:0 third:8:0 turn:14:1 turn:15:1 turn:15:0 "
-            "turn:14:0 second:9:0 third:11:0 second:11:0 third:9:0 second:12:0 third:12:0 second:14:0 "
-            "second:13:0 third:14:0 second:15:0 third:13:0 third:15:0 ",
-            "gh_mul:0:0 q_scale:0:0 c_scale:0:0 c_scale:1:0 c_quant:0:0 q_quant:0:0 q_scale:2:0 "
-            "q_quant:2:0 q_scale:1:0 q_quant:1:0 c_quant:1:0 q_scale:3:0 c_keep:0:0 dist:0:0 dist:4:0 "
-            "q_quant:3:0 c_scale:2:0 y_quant:1:0 c_scale:3:0 c_quant:2:0 c_quant:3:0 q_scale:4:0 "
-            "dist:2:1 dist:2:0 dist:3:1 dist:0:1 dist:6:1 low:0:0 dist:4:1 low:2:0 low:4:0 row_b:2:0 "
-            "dist:1:1 dist:6:0 dist:3:0 dist:1:0 low:3:0 low:1:0 row_b:4:0 dist:5:1 q_quant:4:0 "
-            "row_b:3:0 q_scale:5:0 row_b:1:0 row_b:0:0 low:6:0 dist:7:1 dist:7:0 dist:5:0 row_b:6:0 "
-            "q_quant:5:0 low:7:0 low:5:0 row_b:7:0 dist:10:1 dist:10:0 dist:8:0 row_b:5:0 low:10:0 "
-            "q_scale:6:0 dist:8:1 dist:9:1 q_quant:6:0 q_scale:7:0 dist:11:1 dist:9:0 dist:12:0 "
-            "q_quant:7:0 low:9:0 inv:5:0 inv:1:0 dist:11:0 dist:13:0 dist:13:1 inv:0:0 low:8:0 "
-            "row_b:10:0 dist:12:1 low:13:0 low:11:0 row_b:8:0 unpack:0:1 dist:15:1 inv:3:0 inv:4:0 "
-            "row_b:9:0 inv:2:0 dist:14:1 low:12:0 unpack:1:1 row_b:11:0 row_b:13:0 unpack:0:0 dist:15:0 "
-            "a_quant:0:0 inv:7:0 y_quant:0:0 row_b:12:0 unpack:1:0 inv:6:0 dist:14:0 low:15:0 "
-            "unpack:5:1 low:14:0 unpack:2:0 row_b:15:0 a_quant:1:0 unpack:3:1 row_b:14:0 unpack:2:1 "
-            "unpack:3:0 leave:0:0 a_quant:2:0 unpack:5:0 a_quant:3:0 leave_t:1:0 leave_t:0:0 unpack:4:1 "
-            "a_quant:5:0 leave:1:0 inv:8:0 leave_t:2:0 unpack:4:0 inv:9:0 leave_t:3:0 unpack:7:1 "
-            "a_quant:4:0 inv:10:0 unpack:7:0 unpack:6:1 unpack:6:0 leave:2:0 a_quant:7:0 inv:11:0 "
-            "a_quant:6:0 inv:13:0 unpack:9:0 unpack:8:1 unpack:10:0 unpack:8:0 inv:12:0 unpack:10:1 "
-            "a_quant:8:0 unpack:9:1 a_quant:10:0 unpack:11:1 inv:14:0 unpack:13:1 weigh:14:0 inv:15:0 "
-            "unpack:11:0 unpack:13:0 unpack:12:1 unpack:12:0 o_quant:3:0 a_quant:11:0 a_quant:9:0 "
-            "unpack:14:1 unpack:15:1 o_quant:1:0 a_quant:12:0 unpack:14:0 unpack:15:0 a_quant:14:0 "
-            "o_quant:4:0 a_quant:13:0 o_quant:5:0 o_quant:0:0 a_quant:15:0 leave_t:14:0 leave_t:13:0 "
-            "o_quant:6:0 o_quant:2:0 leave:13:0 o_quant:7:0 ",
-            "g_keep:0:0 c_square:0:0 c_square:1:0 y_group:0:0 q_acc:1:0 c_square:2:0 c_square:3:0 "
-            "q_acc:0:0 y_group:1:0 q_acc:3:0 q_acc:5:0 q_acc:6:0 c_keep:1:0 q_acc:2:0 q_acc:4:0 "
-            "q_acc:7:0 q_acc:8:0 root:2:0 q_acc:9:0 q_acc:11:0 root:4:0 root:0:0 root:1:0 root:3:0 "
-            "q_acc:13:0 q_acc:10:0 root:6:0 root:7:0 row_c:0:0 root:5:0 expo:1:0 expo:5:0 expo:0:0 "
-            "expo:6:0 expo:3:0 expo:2:0 q_acc:14:0 expo:7:0 expo:4:0 q_acc:12:0 q_acc:15:0 root:10:0 "
-            "root:11:0 root:13:0 root:8:0 root:9:0 root:12:0 root:15:0 row_c:1:0 root:14:0 expo:8:0 "
-            "expo:9:0 expo:10:0 leave_t:5:0 leave:3:0 expo:11:0 expo:13:0 leave:5:0 leave_t:4:0 "
-            "expo:12:0 leave:7:0 leave:4:0 expo:14:0 expo:15:0 leave_t:7:0 leave:6:0 leave_t:6:0 "
-            "leave_t:8:0 leave_t:10:0 leave:8:0 leave:10:0 leave_t:9:0 leave:11:0 leave_t:11:0 "
-            "leave:9:0 leave_t:12:0 leave:12:0 leave:14:0 leave_t:15:0 leave:15:0 ",
-            "q_w:1:0 q_w:0:0 q_w:3:0 q_w:6:0 q_w:5:0 q_w:2:0 q_w:4:0 q_w:7:0 q_w:8:0 row_a:0:0 "
-            "row_a:2:0 q_w:9:0 row_a:4:0 q_w:11:0 row_a:3:0 row_a:1:0 q_w:13:0 row_a:6:0 q_w:10:0 "
-            "row_a:7:0 row_a:5:0 q_w:12:0 q_w:15:0 row_a:10:0 q_w:14:0 row_a:9:0 weigh:5:0 weigh:0:0 "
-            "weigh:1:0 row_a:8:0 row_a:11:0 row_a:13:0 row_a:12:0 weigh:2:0 weigh:7:0 weigh:3:0 "
-            "row_a:15:0 weigh:4:0 row_a:14:0 weigh:6:0 weigh:8:0 weigh:9:0 weigh:10:0 weigh:11:0 "
-            "weigh:13:0 weigh:12:0 weigh:15:0 ",
-        ]
         queues = []
-        for text in orders:
+        for order in (ORDER_TENSOR, ORDER_VECTOR, ORDER_SCALAR, ORDER_GPSIMD):
+            seen = {}
             queue = []
-            for word in text.split():
-                name, i, n = word.split(":")
-                queue.append((name, int(i), int(n)))
+            for name in order.split():
+                k = seen.get(name, 0)
+                seen[name] = k + 1
+                if name in ON_VECTOR:
+                    mine = [i for i in range(TILES) if (i in ON_VECTOR[name]) == (order == ORDER_VECTOR)]
+                    k = mine[k]
+                queue.append((name, k))
             queues.append(queue)
-        room = {"x": 4, "o": 4, "og": 8, "art": 6}
-        made, done, at = {}, set(), [0, 0, 0, 0]
-        left = sum([len(z) for z in queues])
-        while left:
-            before = left
-            for k in range(4):
-                while at[k] < len(queues[k]):
-                    f, i, n = queues[k][at[k]]
-                    if not all([d in done for d in reads(f, i, n)]):
+
+        written = set()
+        at = [0 for queue in queues]
+        filled = {tag: [] for tag in ROOM}
+        while len(written) < sum([len(queue) for queue in queues]):
+            before = len(written)
+            for e in range(len(queues)):
+                while at[e] < len(queues[e]):
+                    name, i = queues[e][at[e]]
+                    function, reads, fills = steps[name]
+                    waits = list(reads(i))
+                    for tag, readers in fills(i):
+                        if len(filled[tag]) >= ROOM[tag]:
+                            waits.extend(filled[tag][len(filled[tag]) - ROOM[tag]])
+                    if not all([w in written for w in waits]):
                         break
-                    fresh = fills(f, i, n)
-                    free = True
-                    for e in range(len(fresh)):
-                        tag = fresh[e][0]
-                        m = len(made.setdefault(tag, [])) + e - room.get(tag, 3)
-                        if m >= 0 and not all([d in done for d in made[tag][m]]):
-                            free = False
-                    if not free:
-                        break
-                    for tag, readers in fresh:
-                        made[tag].append(readers)
-                    if f in ("cross", "dist", "turn", "unpack"):
-                        fns[f](i, n)
-                    else:
-                        fns[f](i)
-                    done.add((f, i, n))
-                    at[k] += 1
-                    left -= 1
-                if k == 0:
-                    continue
-            assert left < before, [queues[k][at[k]] if at[k] < len(queues[k]) else 0 for k in range(4)]
+                    for tag, readers in fills(i):
+                        filled[tag].append(readers)
+                    function(i)
+                    written.add((name, i))
+                    at[e] += 1
+            assert len(written) > before, "the orders wait for each other"

from contextlib import ExitStack

import concourse.mybir as mybir
from concourse.masks import make_identity

F32 = mybir.dt.float32
BF16 = mybir.dt.bfloat16
U32 = mybir.dt.uint32
I32 = mybir.dt.int32
U8 = mybir.dt.uint8
FP8X4 = mybir.dt.float8_e4m3fn_x4
ALU = mybir.AluOpType
ACT = mybir.ActivationFunctionType

B, N, E, C = 2048, 1024, 512, 512
P = 128
TILES = B // P
PAIRS = TILES // 2
FLOPS = 2 * B * N * E + 2 * B * N * C

KEEP_BELOW = 0.7
FAR = 2.5e17
TINY = 1e-12
SPOT = 1.5
HALF = 8

ROOM = {
    "bank_a": 4,
    "bank_b": 4,
    "grouped": 3,
    "square": 5,
    "ar": 3,
    "ar_turned": 4,
    "ar_codes": 4,
    "result_grouped": 5,
    "result": 6,
    "result_codes": 8,
}

ORDER_TENSOR = (
    "c_turn c_turn spread c_turn c_turn q_turn c_sum cross0 cross0 q_turn q_turn c_sum c_sum c_sum "
    "cross0 q_turn cross0 cross1 cross1 q_sum q_turn cross1 cross0 q_sum cross1 cross0 cross1 q_turn "
    "cross1 q_sum cross0 cross0 q_turn q_sum cross1 cross1 q_turn cross1 q_sum spread cross0 cross1 "
    "q_sum cross0 cross0 cross1 q_sum cross0 cross0 cross1 cross0 cross1 cross0 q_sum turn cross1 "
    "turn cross0 cross1 turn cross1 second_t second turn second_t second turn second_t turn second_t "
    "turn second second_t second second turn second_t turn turn turn second second second_t second_t "
    "second turn second_t second_t second second_t turn second second second turn turn second "
    "second_t turn second second_t second_t second_t second_t second second"
)
ORDER_VECTOR = (
    "c_scale c_scale c_quant q_scale q_quant c_quant c_scale q_scale q_quant c_keep c_scale c_quant "
    "q_scale c_quant q_quant dist0 dist0 y_quant dist0 q_scale dist0 q_quant dist1 y_quant dist1 "
    "q_keep low dist1 low q_scale q_keep row_inverse dist0 low dist1 dist0 row_inverse dist1 q_scale "
    "q_keep row_inverse q_quant dist0 low dist1 low row_inverse low row_inverse dist0 dist1 dist1 "
    "row_inverse q_keep q_scale low low row_inverse q_keep dist1 dist1 row_inverse q_quant dist0 "
    "dist0 dist0 q_scale low low row_total q_keep dist0 row_inverse dist1 q_quant q_quant weigh "
    "row_total row_inverse dist0 dist1 weigh row_total dist0 q_keep low dist0 dist1 weigh row_inverse "
    "low row_total dist1 dist0 low row_inverse weigh q_keep row_total row_total row_inverse ar_quant "
    "low dist1 ar_quant row_inverse dist1 low low row_total row_inverse weigh row_inverse ar_quant "
    "row_total weigh result_quant weigh ar_quant leave ar_quant weigh leave_t row_total leave_t unpack "
    "row_total weigh row_total ar_quant weigh leave weigh unpack ar_quant ar_quant row_total leave_t "
    "ar_quant weigh unpack leave row_total ar_quant row_total ar_quant leave weigh row_total leave_t "
    "ar_quant weigh weigh row_total ar_quant weigh ar_quant leave leave_t ar_quant result_quant result_quant "
    "ar_quant result_quant result_quant result_quant result_quant leave result_quant"
)
ORDER_SCALAR = (
    "c_squares c_squares c_squares q_square c_squares gain y_group q_square q_square y_group c_keep "
    "q_square q_square root q_square q_square root root q_square root root root gain root row_slope "
    "root expo expo expo expo expo expo expo expo unpack root root root unpack root unpack root "
    "leave_t leave root leave_t unpack root row_slope root unpack expo expo expo leave leave leave_t "
    "expo unpack expo unpack expo leave unpack leave_t leave_t expo unpack leave_t leave expo unpack "
    "leave_t leave unpack leave unpack leave unpack leave leave_t leave_t leave_t leave_t leave"
)
ORDER_GPSIMD = "row_unit " * TILES

ON_VECTOR = {
    "c_keep": [0],
    "unpack": [5, 7, 9],
    "leave": [1, 2, 6, 7, 11, 14],
    "leave_t": [2, 3, 5, 9, 11],
}


def tile_modernncastochasticneighbourregressor_x1_kernel(tc, q, c, g, h, y, u, r, out_0, out_1, out_2):
    nc = tc.nc
    with ExitStack() as ctx:
        keep = ctx.enter_context(tc.tile_pool(name="keep", bufs=1))
        wide = ctx.enter_context(tc.tile_pool(name="wide", bufs=TILES))
        work = ctx.enter_context(tc.tile_pool(name="work", bufs=3))
        psum = ctx.enter_context(tc.psum_pool(name="psum", bufs=4))

        identity = keep.tile([P, P], F32, name="identity")
        make_identity(nc, identity[:])
        ones = keep.tile([P, P], BF16, name="ones")
        ones32 = keep.tile([P, P], F32, name="ones32")
        r_row = keep.tile([P, N], BF16, name="r_row")
        u_row = keep.tile([1, N], BF16, name="u_row")
        far_row = keep.tile([P, N], F32, name="far_row")
        g4 = keep.tile([P, 4], BF16, name="g4")
        h8 = keep.tile([P, 8], BF16, name="h8")
        gh = keep.tile([P, 4], F32, name="gh")
        c_in = keep.tile([P, 2, 4, E], BF16, name="c_in")
        y_in = keep.tile([P, 2, 4, C], BF16, name="y_in")
        q_in = keep.tile([P, TILES, E], BF16, name="q_in")
        r_all = keep.tile([P, N], F32, name="r_all")
        c2 = keep.tile([P, N], F32, name="c2")
        c_square = [keep.tile([P, 4, 512], F32, name="c_square%d" % a) for a in range(2)]
        ch_codes = keep.tile([P, N], U32, name="ch_codes", align_bytes=64)
        ch_scales = keep.tile([P, N], U8, name="ch_scales", align_bytes=64)
        qg_codes = keep.tile([P, B], U32, name="qg_codes", align_bytes=64)
        qg_scales = keep.tile([P, B], U8, name="qg_scales", align_bytes=64)
        y_grouped = keep.tile([P, 2, 4 * C], BF16, name="y_grouped", align_bytes=64)
        y_codes = keep.tile([P, 2, C], U32, name="y_codes", align_bytes=64)
        y_scales = keep.tile([P, 2, C], U8, name="y_scales", align_bytes=64)
        result_scales = keep.tile([P, B], U8, name="result_scales", align_bytes=64)
        q2 = keep.tile([P, TILES], F32, name="q2")
        least = keep.tile([P, TILES], F32, name="least")
        unit = keep.tile([P, TILES], F32, name="unit")
        per_unit = keep.tile([P, TILES], F32, name="per_unit")
        slope = keep.tile([P, TILES], F32, name="slope")
        minus_slope = keep.tile([P, TILES], F32, name="minus_slope")
        shift = keep.tile([P, TILES], F32, name="shift")
        total = keep.tile([P, TILES], F32, name="total")
        per_total = keep.tile([P, TILES], F32, name="per_total")
        x = [wide.tile([P, N], F32, name="x") for i in range(TILES)]

        ctx.enter_context(tc.manual_schedule())

        nc.scalar.dma_start(out=h8[:, 0:4], in_=h.rearrange("(p t) -> p t", t=4))
        nc.scalar.dma_start(out=g4[:], in_=g.rearrange("(p t) -> p t", t=4))
        nc.scalar.dma_start(out=u_row[:], in_=u.unsqueeze(0))
        nc.gpsimd.memset(far_row[:], 0.0)
        nc.vector.memset(ones32[:], 1.0)
        nc.vector.memset(r_row[:].bitcast(I32), 0)
        nc.vector.memset(ones[:], 1.0)
        nc.scalar.dma_start(out=r_row[0:1, :], in_=r.unsqueeze(0))
        c_view = c.rearrange("(a p t) d -> a p t d", a=2, t=4)
        q_view = q.rearrange("(k p) d -> p k d", p=P)
        y_view = y.rearrange("(a p t) d -> a p t d", a=2, t=4)
        for a in range(2):
            for v in range(2):
                nc.sync.dma_start(out=c_in[:, a, 2 * v : 2 * v + 2, :], in_=c_view[a, :, 2 * v : 2 * v + 2, :])
        for j in range(PAIRS):
            nc.sync.dma_start(out=q_in[:, 2 * j : 2 * j + 2, :], in_=q_view[:, 2 * j : 2 * j + 2, :])
            if j == PAIRS // 2 - 1:
                for a in range(2):
                    nc.sync.dma_start(out=y_in[:, a, :, :], in_=y_view[a])
        nc.vector.tensor_copy(out=h8[:, 4:8], in_=h8[:, 0:4])
        nc.vector.tensor_tensor(out=gh[:], in0=g4[:], in1=h8[:, 0:4], op=ALU.mult)
        for a in range(2):
            for v in range(2):
                s = 512 * a + 256 * v
                nc.vector.tensor_scalar(
                    out=far_row[0:1, s : s + 256].rearrange("p (e c) -> p e c", e=2),
                    in0=u_row[:, 512 * a : 512 * a + 512].rearrange("p (c v e) -> p v e c", v=2, e=2)[:, v, :, :],
                    scalar1=KEEP_BELOW,
                    scalar2=FAR,
                    op0=ALU.is_ge,
                    op1=ALU.mult,
                )

        made = {}

        def bank(tag, *key):
            made[key] = psum.tile([P, 512], F32, name=tag, bufs=ROOM[tag])
            return made[key]

        def rotating(tag, shape, dtype, *key):
            made[key] = work.tile(shape, dtype, name=tag, bufs=ROOM[tag], align_bytes=64)
            return made[key]


        def spread(a):
            t = bank("bank_a", "spread", a)
            nc.tensor.matmul(t[:], lhsT=ones[:], rhs=r_row[:, 512 * a : 512 * a + 512], start=True, stop=True)

        def gain(a):
            nc.scalar.copy(
                out=r_all[:, 512 * a : 512 * a + 512].rearrange("p (v c e) -> p v c e", v=2, e=2),
                in_=made["spread", a][:].rearrange("p (c v e) -> p v c e", v=2, e=2),
            )


        def c_turn(k):
            t = bank("bank_b", "c", k)
            for e in range(2):
                words = c_in[:, k // 2, 2 * (k % 2) + e, :].bitcast(F32)
                for w in range(2):
                    s = (2 * e + w) * P
                    nc.tensor.transpose(t[:, s : s + P], words[:, w : E // 2 : 2], identity[:])

        def c_scale(k):
            t = rotating("grouped", [P, 1024], BF16, "ch", k)
            nc.vector.tensor_tensor(
                out=t[:].rearrange("p (c x d) -> p c x d", x=4, d=2),
                in0=made["c", k][:].bitcast(BF16).rearrange("p (x c d) -> p c x d", x=4, d=2),
                in1=h8[:].rearrange("p (x d) -> p x d", d=2).unsqueeze(1).to_broadcast([P, P, 4, 2]),
                op=ALU.mult,
            )

        def c_squares(k):
            bits = made["c", k][:].bitcast(BF16).rearrange("p (e w c d) -> p w e c d", e=2, w=2, d=2)
            s = slice(256 * (k % 2), 256 * (k % 2) + 256)
            for d in range(2):
                nc.scalar.activation(
                    out=c_square[k // 2][:, d:4:2, s].rearrange("p w (e c) -> p w e c", e=2),
                    in_=bits[:, :, :, :, d],
                    func=ACT.Square,
                )

        def c_quant(k):
            s = slice(256 * k, 256 * k + 256)
            nc.vector.quantize_mx(out=ch_codes[:, s].bitcast(FP8X4), scales=ch_scales[:, s], in_=made["ch", k][:])

        def c_sum(k):
            a = k // 2
            if ("c2", a) not in made:
                bank("bank_a", "c2", a)
            s = slice(256 * (k % 2), 256 * (k % 2) + 256)
            t = made["c2", a]
            nc.tensor.matmul(t[:, s], lhsT=ones32[:], rhs=far_row[:, 256 * k : 256 * k + 256], start=True, stop=False)
            for m in range(4):
                nc.tensor.matmul(
                    t[:, s],
                    lhsT=gh[:, m : m + 1].to_broadcast([P, P]),
                    rhs=c_square[a][:, m, s],
                    start=False,
                    stop=(m == 3),
                )

        def c_keep(a):
            copy = nc.vector.tensor_copy if a in ON_VECTOR["c_keep"] else nc.scalar.copy
            copy(
                out=c2[:, 512 * a : 512 * a + 512].rearrange("p (v c e) -> p v c e", v=2, e=2),
                in_=made["c2", a][:].rearrange("p (v e c) -> p v c e", v=2, e=2),
            )


        def q_turn(j):
            t = bank("bank_b", "q", j)
            for w in range(2):
                for k in range(2):
                    s = w * 256 + k * P
                    words = q_in[:, 2 * j + k, :].bitcast(F32)
                    nc.tensor.transpose(t[:, s : s + P], words[:, w : E // 2 : 2], identity[:])

        def q_scale(j):
            t = rotating("grouped", [P, 1024], BF16, "qg", j)
            nc.vector.tensor_tensor(
                out=t[:].rearrange("p (b w d) -> p b w d", w=2, d=2),
                in0=made["q", j][:].bitcast(BF16).rearrange("p (w b d) -> p b w d", w=2, d=2),
                in1=g4[:].rearrange("p (w d) -> p w d", d=2).unsqueeze(1).to_broadcast([P, 256, 2, 2]),
                op=ALU.mult,
            )

        def q_square(j):
            bits = made["q", j][:].bitcast(BF16).rearrange("p (w b d) -> p w b d", w=2, d=2)
            t = rotating("square", [P, 4, 256], F32, "q_square", j)
            for d in range(2):
                nc.scalar.activation(out=t[:, d:4:2, :], in_=bits[:, :, :, d], func=ACT.Square)

        def q_quant(j):
            s = slice(256 * j, 256 * j + 256)
            nc.vector.quantize_mx(out=qg_codes[:, s].bitcast(FP8X4), scales=qg_scales[:, s], in_=made["qg", j][:])

        def q_sum(j):
            t = bank("bank_b", "q2", j)
            for k in range(2):
                for m in range(4):
                    nc.tensor.matmul(
                        t[:, k : k + 1],
                        lhsT=made["q_square", j][:, m, k * P : k * P + P],
                        rhs=gh[:, m : m + 1],
                        start=(m == 0),
                        stop=(m == 3),
                    )

        def q_keep(j):
            nc.vector.tensor_copy(out=q2[:, 2 * j : 2 * j + 2], in_=made["q2", j][:, 0:2])


        def cross(i, n):
            t = bank("bank_a", "cross", i, n)
            b = slice(P * i, P * i + P)
            s = slice(512 * n, 512 * n + 512)
            nc.tensor.matmul_mx(
                out=t[:],
                lhsT=qg_codes[:, b].bitcast(FP8X4),
                lhsT_scale=qg_scales[:, b],
                rhs=ch_codes[:, s].bitcast(FP8X4),
                rhs_scale=ch_scales[:, s],
                start=True,
                stop=True,
            )

        def dist(i, n):
            s = slice(512 * n, 512 * n + 512)
            nc.vector.scalar_tensor_tensor(
                out=x[i][:, s], in0=made["cross", i, n][:], scalar=-2.0, in1=c2[:, s], op0=ALU.mult, op1=ALU.add
            )

        def low(i):
            nc.vector.tensor_scalar(
                out=x[i][:],
                in0=x[i][:],
                scalar1=q2[:, i : i + 1],
                scalar2=None,
                op0=ALU.add,
                op1=ALU.min,
                accum_out=least[:, i : i + 1],
            )

        def row_unit(i):
            s = slice(i, i + 1)
            nc.gpsimd.tensor_scalar(
                out=unit[:, s], in0=least[:, s], scalar1=TINY, scalar2=1.0 / SPOT, op0=ALU.max, op1=ALU.mult
            )

        def row_inverse(i):
            nc.vector.reciprocal(out=per_unit[:, i : i + 1], in_=unit[:, i : i + 1])

        def root(i):
            nc.scalar.activation(out=x[i][:], in_=x[i][:], func=ACT.Sqrt, scale=per_unit[:, i : i + 1])

        def row_slope(k):
            s = slice(0, HALF) if k == 0 else slice(HALF, TILES)
            nc.scalar.activation(out=slope[:, s], in_=unit[:, s], func=ACT.Sqrt, scale=4.0)
            nc.gpsimd.tensor_scalar(
                out=minus_slope[:, s], in0=slope[:, s], scalar1=-1.0, scalar2=0.0, op0=ALU.mult, op1=ALU.add
            )
            nc.gpsimd.tensor_scalar(
                out=shift[:, s], in0=slope[:, s], scalar1=SPOT**0.5, scalar2=0.0, op0=ALU.mult, op1=ALU.add
            )

        def expo(i):
            nc.scalar.activation(
                out=x[i][:],
                in_=x[i][:],
                func=ACT.Exp,
                scale=minus_slope[:, i : i + 1],
                bias=shift[:, i : i + 1],
                accum_out=total[:, i : i + 1],
            )

        def row_total(i):
            nc.vector.reciprocal(out=per_total[:, i : i + 1], in_=total[:, i : i + 1])


        def y_group(a):
            nc.scalar.copy(
                out=y_grouped[:, a, :].rearrange("p (m c t) -> p m c t", m=4, t=4),
                in_=y_in[:, a, :, :].rearrange("p t (c m) -> p m c t", m=4),
            )

        def y_quant(a):
            nc.vector.quantize_mx(
                out=y_codes[:, a, :].bitcast(FP8X4), scales=y_scales[:, a, :], in_=y_grouped[:, a, :]
            )


        def weigh(i):
            t = rotating("ar", [P, N], BF16, "ar", i)
            nc.vector.scalar_tensor_tensor(
                out=t[:], in0=x[i][:], scalar=per_total[:, i : i + 1], in1=r_all[:], op0=ALU.mult, op1=ALU.mult
            )

        def turn(i):
            t = bank("bank_a", "ar_bank", i)
            words = made["ar", i][:].bitcast(F32)
            for k in range(4):
                nc.tensor.transpose(t[:, P * k : P * k + P], words[:, P * k : P * k + P], identity[:])

        def unpack(i):
            t = rotating("ar_turned", [P, 1024], BF16, "ar_turned", i)
            copy = nc.vector.tensor_copy if i in ON_VECTOR["unpack"] else nc.scalar.copy
            copy(
                out=t[:].bitcast(F32).rearrange("p (a b v) -> p a b v", a=2, v=2),
                in_=made["ar_bank", i][:].rearrange("p (a v b) -> p a b v", a=2, v=2),
            )

        def ar_quant(i):
            codes = rotating("ar_codes", [P, 256], U32, "ar_codes", i)
            scales = work.tile([P, 256], U8, name="ar_scales", bufs=ROOM["ar_codes"], align_bytes=64)
            made["ar_scales", i] = scales
            nc.vector.quantize_mx(out=codes[:].bitcast(FP8X4), scales=scales[:], in_=made["ar_turned", i][:])

        def second_t(i):
            t = bank("bank_b", "result_t_bank", i)
            codes, scales = made["ar_codes", i], made["ar_scales", i]
            for m in range(4):
                s = slice(P * m, P * m + P)
                for a in range(2):
                    k = slice(P * a, P * a + P)
                    nc.tensor.matmul_mx(
                        out=t[:, s],
                        lhsT=y_codes[:, a, s].bitcast(FP8X4),
                        lhsT_scale=y_scales[:, a, s],
                        rhs=codes[:, k].bitcast(FP8X4),
                        rhs_scale=scales[:, k],
                        start=(a == 0),
                        stop=(a == 1),
                    )

        def second(i):
            t = bank("bank_b", "result_bank", i)
            codes, scales = made["ar_codes", i], made["ar_scales", i]
            for a in range(2):
                k = slice(P * a, P * a + P)
                nc.tensor.matmul_mx(
                    out=t[:],
                    lhsT=codes[:, k].bitcast(FP8X4),
                    lhsT_scale=scales[:, k],
                    rhs=y_codes[:, a, :].bitcast(FP8X4),
                    rhs_scale=y_scales[:, a, :],
                    start=(a == 0),
                    stop=(a == 1),
                )

        def leave(i):
            t = rotating("result", [P, C], F32, "result", i)
            copy = nc.vector.tensor_copy if i in ON_VECTOR["leave"] else nc.scalar.copy
            copy(out=t[:].rearrange("p (c m) -> p c m", m=4), in_=made["result_bank", i][:].rearrange("p (m c) -> p c m", m=4))
            nc.sync.dma_start(out=out_0[P * i : P * i + P, :], in_=t[:])

        def leave_t(i):
            if ("result_grouped", i // 2) not in made:
                rotating("result_grouped", [P, 1024], BF16, "result_grouped", i // 2)
            s = slice(512 * (i % 2), 512 * (i % 2) + 512)
            copy = nc.vector.tensor_copy if i in ON_VECTOR["leave_t"] else nc.scalar.copy
            copy(
                out=made["result_grouped", i // 2][:, s].rearrange("p (b m) -> p b m", m=4),
                in_=made["result_t_bank", i][:].rearrange("p (m b) -> p b m", m=4),
            )

        def result_quant(j):
            t = rotating("result_codes", [P, 256], U32, "result_codes", j)
            s = slice(256 * j, 256 * j + 256)
            nc.vector.quantize_mx(out=t[:].bitcast(FP8X4), scales=result_scales[:, s], in_=made["result_grouped", j][:])
            nc.sync.dma_start(
                out=out_1[0, :, s, :].rearrange("p m t -> p (m t)").bitcast(I32), in_=t[:].bitcast(I32)
            )
            if j % 4 == 3:
                s = slice(256 * (j - 3), 256 * j + 256)
                for b in range(4):
                    nc.sync.dma_start(
                        out=out_2[0, 4 * b : 4 * b + 4, s].bitcast(I32), in_=result_scales[32 * b : 32 * b + 4, s].bitcast(I32)
                    )

        def both(name, i):
            return [(name, 2 * i), (name, 2 * i + 1)]

        def nothing(i):
            return []

        steps = {
            "spread": (spread, nothing, lambda i: [("bank_a", [("gain", i)])]),
            "gain": (gain, lambda i: [("spread", i)], nothing),
            "c_turn": (c_turn, nothing, lambda i: [("bank_b", [("c_scale", i), ("c_squares", i)])]),
            "c_scale": (c_scale, lambda i: [("c_turn", i)], lambda i: [("grouped", [("c_quant", i)])]),
            "c_squares": (c_squares, lambda i: [("c_turn", i)], nothing),
            "c_quant": (c_quant, lambda i: [("c_scale", i)], nothing),
            "c_sum": (c_sum, lambda i: [("c_squares", i)], lambda i: [("bank_a", [("c_keep", i // 2)])] if i % 2 == 0 else []),
            "c_keep": (c_keep, lambda i: both("c_sum", i), nothing),
            "q_turn": (q_turn, nothing, lambda i: [("bank_b", [("q_scale", i), ("q_square", i)])]),
            "q_scale": (q_scale, lambda i: [("q_turn", i)], lambda i: [("grouped", [("q_quant", i)])]),
            "q_square": (q_square, lambda i: [("q_turn", i)], lambda i: [("square", [("q_sum", i)])]),
            "q_quant": (q_quant, lambda i: [("q_scale", i)], nothing),
            "q_sum": (q_sum, lambda i: [("q_square", i)], lambda i: [("bank_b", [("q_keep", i)])]),
            "q_keep": (q_keep, lambda i: [("q_sum", i)], nothing),
            "cross0": (
                lambda i: cross(i, 0),
                lambda i: [("q_quant", i // 2)] + both("c_quant", 0),
                lambda i: [("bank_a", [("dist0", i)])],
            ),
            "cross1": (
                lambda i: cross(i, 1),
                lambda i: [("q_quant", i // 2)] + both("c_quant", 1),
                lambda i: [("bank_a", [("dist1", i)])],
            ),
            "dist0": (lambda i: dist(i, 0), lambda i: [("cross0", i), ("c_keep", 0)], nothing),
            "dist1": (lambda i: dist(i, 1), lambda i: [("cross1", i), ("c_keep", 1)], nothing),
            "low": (low, lambda i: [("dist0", i), ("dist1", i), ("q_keep", i // 2)], nothing),
            "row_unit": (row_unit, lambda i: [("low", i)], nothing),
            "row_inverse": (row_inverse, lambda i: [("row_unit", i)], nothing),
            "root": (root, lambda i: [("row_inverse", i)], nothing),
            "row_slope": (
                row_slope,
                lambda k: [("row_unit", i) for i in (range(HALF) if k == 0 else range(HALF, TILES))],
                nothing,
            ),
            "expo": (expo, lambda i: [("root", i), ("row_slope", 0 if i < HALF else 1)], nothing),
            "row_total": (row_total, lambda i: [("expo", i)], nothing),
            "y_group": (y_group, nothing, nothing),
            "y_quant": (y_quant, lambda i: [("y_group", i)], nothing),
            "weigh": (
                weigh,
                lambda i: [("row_total", i)] + both("gain", 0),
                lambda i: [("ar", [("turn", i)])],
            ),
            "turn": (turn, lambda i: [("weigh", i)], lambda i: [("bank_a", [("unpack", i)])]),
            "unpack": (unpack, lambda i: [("turn", i)], lambda i: [("ar_turned", [("ar_quant", i)])]),
            "ar_quant": (
                ar_quant,
                lambda i: [("unpack", i)],
                lambda i: [("ar_codes", [("second_t", i), ("second", i)])],
            ),
            "second_t": (
                second_t,
                lambda i: [("ar_quant", i)] + both("y_quant", 0),
                lambda i: [("bank_b", [("leave_t", i)])],
            ),
            "second": (
                second,
                lambda i: [("ar_quant", i)] + both("y_quant", 0),
                lambda i: [("bank_b", [("leave", i)])],
            ),
            "leave": (leave, lambda i: [("second", i)], nothing),
            "leave_t": (
                leave_t,
                lambda i: [("second_t", i)] + ([("leave_t", i - 1)] if i % 2 else []),
                lambda i: [("result_grouped", [("result_quant", i // 2)])] if i % 2 == 0 else [],
            ),
            "result_quant": (result_quant, lambda i: both("leave_t", i), nothing),
        }

        queues = []
        for order in (ORDER_TENSOR, ORDER_VECTOR, ORDER_SCALAR, ORDER_GPSIMD):
            seen = {}
            queue = []
            for name in order.split():
                k = seen.get(name, 0)
                seen[name] = k + 1
                if name in ON_VECTOR:
                    mine = [i for i in range(TILES) if (i in ON_VECTOR[name]) == (order == ORDER_VECTOR)]
                    k = mine[k]
                queue.append((name, k))
            queues.append(queue)

        written = set()
        at = [0 for queue in queues]
        filled = {tag: [] for tag in ROOM}
        while len(written) < sum([len(queue) for queue in queues]):
            before = len(written)
            for e in range(len(queues)):
                while at[e] < len(queues[e]):
                    name, i = queues[e][at[e]]
                    function, reads, fills = steps[name]
                    waits = list(reads(i))
                    for tag, readers in fills(i):
                        if len(filled[tag]) >= ROOM[tag]:
                            waits.extend(filled[tag][len(filled[tag]) - ROOM[tag]])
                    if not all([w in written for w in waits]):
                        break
                    for tag, readers in fills(i):
                        filled[tag].append(readers)
                    function(i)
                    written.add((name, i))
                    at[e] += 1
            assert len(written) > before, "the orders wait for each other"
